import numpy as np, ml_dtypes
CORES = [5,29,101,125,133,157,229,253]
N = 8
BF = ml_dtypes.bfloat16
S, F, L, RO, A, TH, BYG = 2048, 624, 208, 3, 544, 9, 0
def whole(x, hi):
    return np.minimum(x.astype(np.int64), hi)
def parts(rng):
    a = rng.choice(np.array([0.2, 0.3, 0.4, 0.5]), (N, 8, 1, 1)).astype(np.float32)
    t = whole(256 * rng.random((N, 8, 16, S), dtype=np.float32) ** a, 255)
    t = np.where(rng.random((N, 8, 1, S)) < 0.25, 255, t)
    return t, rng.integers(0, 255, (N, 8, 16, F)), rng.integers(0, S, (N, 8, 16, F)), rng.integers(0, S, (N, 8, 16, F))
def pack(t, z, eh, ef):
    return {"tab": t.reshape(N, 128, S).astype(np.float32).astype(BF), "zf": z.reshape(N, 128, F).astype(np.float32).astype(BF),
            "eh": np.ascontiguousarray(eh.reshape(N, 128, F)).astype(np.int32), "ef": np.ascontiguousarray(ef.reshape(N, 128, F)).astype(np.int32)}
def setup_inputs(rng):
    return pack(*parts(rng))
def setup_inputs_full(rng):
    t, z, eh, ef = parts(rng)
    for g in (0, 5):
        t[:, g] = 255; eh[:, g] = rng.integers(F, S, (N, 16, F)); ef[:, g] = rng.integers(F, S, (N, 16, F))
        eh[:, g, 0] = np.argsort(rng.random((N, F)), axis=1)
    f = np.arange(F); c = F - A; see = (f >= A - c) & (f < A)
    m = np.flatnonzero(see)
    for g in (2, 7):
        p = np.argsort(rng.random((N, S // 2)), axis=1)[:, :L]
        t[:, g] = 255; eh[:, g] = rng.integers(S // 2, S - 64, (N, 16, F)); ef[:, g] = rng.integers(S // 2, S - 64, (N, 16, F))
        z[:, g] = np.where(f < L, rng.integers(160, 255, (N, 16, F)), np.where(see, rng.integers(100, 160, (N, 16, F)), rng.integers(0, 100, (N, 16, F))))
        eh[:, g, 0] = np.where(see, eh[:, g, 0], p[:, f % L])
        for r in range(N):
            q = (r + 1 + (2 + BYG * g) % (N - 1)) % N
            a, b = m[1::4], m[3::4]
            ef[r, g, rng.integers(0, 16, len(a)), a] = p[q, L - c - 1]
            ef[r, g, rng.integers(0, 16, len(b)), b] = np.max(p[q])
    return pack(t, z, eh, ef)
def setup_inputs_ties(rng):
    t, z, eh, ef = parts(rng)
    pat = np.array([0, 0, 2, 3, 5, TH - 2, TH - 2, TH - 2, TH - 1, TH - 1, TH - 1, TH - 1, TH, TH, TH, 16])
    place = np.argsort(rng.random((N, 4, 16, S), dtype=np.float32), axis=2)
    t[:, :4] = np.where(place < pat[np.arange(S) % 16], 0, 255)
    for x in (eh, ef):
        top = rng.choice(np.array([8, 12, 12, 12, 15, 16]), (N, 4, 1, F))
        x[:, :4] = 16 * rng.integers(0, S // 16, (N, 4, 16, F)) + (rng.random((N, 4, 16, F)) * top).astype(np.int64)
    v = np.array([0, 1, 127, 128, 254, 255])
    t[:, 4:] = rng.choice(v, (N, 4, 16, S), p=[0.04, 0.04, 0.1, 0.12, 0.3, 0.4]); z[:, 4:] = rng.choice(v[:5], (N, 4, 16, F))
    return pack(t, z, eh, ef)
def setup_inputs_alike(rng):
    t, z, eh, ef = parts(rng); few = np.array([0, S - 1, S // 2, 3])
    eh[:, 0] = rng.choice(few, (N, 16, F)); eh[:, 1] = rng.integers(0, S, (N, 1, F))
    t[:, 2] = 255; eh[:, 2] = rng.integers(0, S, (N, 1, 1))
    eh[:, 3] = S - 1 - rng.integers(0, 12, (N, 16, F)); ef[:, 3] = S - 1 - rng.integers(0, 12, (N, 16, F))
    ef[:, 4] = rng.choice(few, (N, 16, F))
    for x in (z, eh, ef): x[:, 5, :, 1::2] = x[:, 5, :, 0::2]
    return pack(t, z, eh, ef)
def setup_inputs_hard(rng):
    t, z, eh, ef = parts(rng)
    t[:, 0] = 0; t[rng.integers(0, N), 1] = 0; t[:, 2] = 255
    z[:, 3] = 0; t[:, 3] = np.maximum(t[:, 3], 1)
    z[:, 4] = 254; t[:, 4] = np.where(rng.random((N, 16, S)) < 0.8, 255, t[:, 4])
    return pack(t, z, eh, ef)
def setup_inputs_spread(rng):
    u = np.float32(2) ** -rng.integers(-2, 6, (N, 8, 1, S)).astype(np.float32); v = np.float32(2) ** rng.integers(-2, 5, (N, 8, 1, F)).astype(np.float32)
    t = whole(256 * rng.random((N, 8, 16, S), dtype=np.float32) ** u, 255); z = whole(255 * rng.random((N, 8, 16, F), dtype=np.float32) ** v, 254)
    e = [whole(S * rng.random((N, 8, 16, F)) ** (2.0 ** rng.integers(0, 3, (N, 8, 16, 1))), S - 1) for i in range(2)]
    return pack(t, z, e[0], e[1])
def check_inputs(d):
    bad = []
    for k, hi in (("tab", 255), ("zf", 254), ("eh", S - 1), ("ef", S - 1)):
        v = np.asarray(d[k]).astype(np.float64)
        if not (np.min(v) >= 0 and np.max(v) <= hi): bad.append("range of " + k)
        if not np.all(v == np.floor(v)): bad.append("whole numbers in " + k)
    return bad
def reference(tab, zf, eh, ef):
    t = tab.astype(np.float32).astype(np.int32).reshape(N, 8, 16, S); z = zf.astype(np.float32).astype(np.int32).reshape(N, 8, 16, F)
    home = eh.astype(np.int64).reshape(N, 8, 16, F); far = ef.astype(np.int64).reshape(N, 8, 16, F)
    d = np.zeros((N, 8, F), np.int64); oc = np.full((N, 8, S), -1, np.int64); free = np.ones((N, 8, F), bool)
    for step in range(RO):
        old = np.array(t)
        turn = (np.arange(F) + A * step) % F
        for r in range(N):
            for g in range(8):
                q = (r + 1 + (step + BYG * g) % (N - 1)) % N
                ln = turn[free[r, g][turn]][:L]
                zl = z[r, g][:, ln]
                sh = (home[r, g][:, ln] + d[r, g, ln]) & (S - 1); sf = (far[r, g][:, ln] + d[r, g, ln]) & (S - 1)
                ph = np.sum(old[r, g][:, sh] <= zl[:, None, :], axis=0); pf = np.sum(old[q, g][:, sf] <= zl[:, None, :], axis=0)
                k = np.argmax(ph, axis=0)
                worst = np.maximum(np.max(ph, axis=0), np.max(pf, axis=0)); go = worst < TH
                d[r, g, ln] += np.where(go, 0, worst)
                cl = np.flatnonzero(go)
                s, first = np.unique(sh[k, np.arange(L)][cl], return_index=True)
                w = cl[first]; was = oc[r, g, s]; was = was[was >= 0]
                d[r, g, was] += 1; free[r, g, was] = True
                t[r, g][:, s] = zl[:, w]; oc[r, g, s] = ln[w]; free[r, g, ln[w]] = False
    return {"yt": t.reshape(N, 128, S).astype(np.float32).astype(BF), "yo": oc.astype(np.float32), "yd": d.astype(np.float32)}

@@ -1,0 +1,591 @@
+import math
+from concourse.mybir import AluOpType, ActivationFunctionType
+OP = AluOpType
+AF = ActivationFunctionType
+F32, BF, I32, U16 = "float32", "bfloat16", "int32", "uint16"
+F, L, S = 624, 208, 2048
+WT = S + 3 * 256
+PEN = 32768
+OKB = 8 * PEN
+NB = 112
+LN2 = math.log(2.0)
+
+ENG = "VAPG"
+LOADS = ["ef0", "eh0", "zf0", "tab", "tc", "ef1", "eh1", "zf1"]
+MSGS = ["RQZ", "RQL", "KFR", "F2", "F3", "U2Z", "U2D", "U3Z", "U3D", "V3Z", "V3D"]
+TO = {"RQZ": 1, "RQL": 1, "KFR": -1, "F2": -2, "U2Z": -2, "U2D": -2, "F3": -3, "U3Z": -3, "U3D": -3, "V3Z": -3, "V3D": -3}
+ORDER = ["RQZ", "U3Z", "RQL", "F3", "KFR", "U3D", "V3Z", "V3D"]
+TABLES = ("F2", "F3")
+STORES = ["yt", "yo", "yd"]
+SEMAPHORES = (["q" + e for e in ENG] + ["d_" + n for n in LOADS] + ["o_" + n for n in STORES]
+              + ["a_" + n for n in MSGS] + ["l_" + n for n in MSGS])
+
+SCRATCH = {}
+PLACE = {}
+_fill = {F32: 0, BF: 0, I32: 0, U16: 0}
+
+
+def _sb(name, shape, dtype):
+    if len(shape) == 1 and shape[0] <= 48 and name not in MSGS + ["KFO", "DT0", "DT1"]:
+        PLACE[name] = ("S" + dtype, _fill[dtype], shape[0])
+        _fill[dtype] += -(-shape[0] // 16) * 16
+        return
+    SCRATCH[name] = ("sbuf", [128] + shape, dtype)
+    PLACE[name] = (name, 0, shape[0])
+
+
+for _n, _s, _d in (
+        ("HT", [WT], BF), ("F2", [WT], BF), ("F3", [WT], BF), ("TC", [S], BF), ("OC", [WT], F32),
+        ("ZF", [F], BF), ("EHI", [F], I32), ("EFI", [F], I32), ("EE", [F], F32), ("D", [F], BF), ("DF", [F], F32),
+        ("XE", [128], F32), ("DQ", [128], F32), ("I3", [13, 32], F32), ("Y3", [13, 32], F32), ("XI", [13, 16], I32),
+        ("HF", [2, L], I32), ("GA0", [512], BF), ("GA1", [512], BF), ("GA2", [512], BF),
+        ("CMH", [3328], BF), ("CMF", [3328], BF), ("ZR", [13, 256], BF),
+        ("RQZ", [L], BF), ("RQL", [L], U16), ("KFR", [16], F32), ("KFO", [16], F32),
+        ("U2Z", [L], BF), ("U2D", [16], U16), ("U3Z", [L], BF), ("U3D", [16], U16), ("V3Z", [L], BF), ("V3D", [16], U16),
+        ("HK", [L], F32), ("HS", [L], F32), ("FS", [L], F32), ("HKI", [16], I32), ("HSL", [16], I32), ("A1", [16], F32),
+        ("AP", [16], F32), ("YY", [16], F32), ("IX", [16], U16), ("D0", [16], F32), ("L1", [16], F32), ("D2", [16], F32),
+        ("WM", [16], F32), ("WI", [16], I32), ("WS", [16], I32), ("WR", [16], F32), ("WV", [16], F32), ("WN", [16], F32),
+        ("XB", [L], BF), ("B0", [L], BF), ("B1", [L], BF), ("E0", [13, 128], BF), ("E1", [6, 128], BF),
+        ("NU", [32], F32), ("UU", [32], BF), ("UC", [32], BF), ("QQ", [32], F32), ("TB", [1], F32), ("TU", [1], F32),
+        ("XM", [128], F32), ("XS", [128], F32), ("LVF", [1024], F32), ("LVW", [1024], F32), ("UF", [336], BF),
+        ("GW", [336], BF), ("BP", [336], BF), ("NB1", [L], F32), ("B2", [336], BF), ("B3", [L], F32), ("DL", [128], F32),
+        ("ND", [128], F32),
+        ("PI", [1], I32), ("PJ", [1], I32), ("PK", [1], I32), ("PM", [1], F32), ("MH0", [1], F32), ("MH1", [1], F32),
+        ("PW", [1], F32), ("PX", [1], I32), ("PY", [1], F32), ("ML", [4], F32), ("MH", [4], F32), ("MB", [2], F32),
+        ("KIO", [L], F32), ("M16", [L], F32), ("RKM", [L], F32), ("KAD", [L], F32), ("C16", [32], F32), ("FW", [32], F32),
+        ("DMF", [32], F32), ("ONB", [128], BF), ("BA", [128], BF), ("BO", [128], BF), ("NBO", [128], BF), ("NT", [128], BF),
+        ("ID", [128], BF), ("WMU", [144], BF), ("EX0", [16], F32), ("EX1", [16], F32), ("W0", [16], BF), ("W1", [16], BF),
+        ("THR", [1], F32), ("CL", [264], F32), ("CI", [264], I32), ("CJ", [264], I32), ("CB", [264], F32),
+        ("LB", [2, 256], BF), ("HB", [2, 8], F32), ("CT0", [S + 64], BF), ("CT1", [S + 64], BF),
+        ("F2V", [416], F32), ("L128", [128], F32), ("BLF", [16], F32), ("BL", [16], U16), ("ON32", [32], F32),
+):
+    _sb(_n, _s, _d)
+for _t in range(3):
+    for _n, _s, _d in (("LI", [2, L], U16), ("KA", [L], F32), ("ZL", [L], BF), ("Z16", [13, 256], BF),
+                       ("DU", [16], F32), ("DS", [16], F32), ("DT", [16], U16), ("LW", [80 + 1024], F32),
+                       ("PL", [32], U16), ("LU", [16], U16)):
+        if not (_t == 0 and _n in ("ZL", "LW", "PL", "LU")):
+            _sb("%s%d" % (_n, _t), _s, _d)
+for _d, _w in _fill.items():
+    SCRATCH["S" + _d] = ("sbuf", [128, _w], _d)
+for _n in ["PH", "PF"] + ["T%d" % i for i in range(6)]:
+    SCRATCH[_n] = ("psum", [128, 512], F32)
+    PLACE[_n] = (_n, 0, 512)
+
+
+def plan(T, topo):
+    n = len(T.cores)
+    out = {}
+    for r in range(n):
+        src = T.cores[r]
+        for m in MSGS:
+            dst = T.cores[(r + TO[m]) % n]
+            relay = None
+            if not topo.may_write(src, dst):
+                c = [x for x in topo.cores_of(src) if x != src and topo.may_write(x, dst) and topo.die(x) == topo.die(src)]
+                relay = c[0] if m == "F3" else c[-1]
+            out[(r, m)] = (src, relay, dst)
+    return out
+
+
+def engines(topo, a, b, m):
+    e = topo.engines(a, b)
+    if m in TABLES:
+        return e[:4] if len(e) == 8 else e[8:12]
+    return e[4:8]
+
+
+def bits(e):
+    return sum(1 << x for x in e)
+
+
+def land(T, m):
+    return T[m][:, 0:S] if m in TABLES else T[m][:, :]
+
+
+def relay_program(g, core, T, topo, pl):
+    todo = sorted((ORDER.index(m), m, r) for (r, m), (s, y, d) in pl.items() if y == core)
+    for _, m, r in todo:
+        s, y, d = pl[(r, m)]
+        g.wait_ge(T.sem["a_" + m], len(engines(topo, s, y, m)))
+        rid, pid = topo.addr(d, y)
+        g.remote_dma(land(T, m), land(T, m), T.sem["a_" + m], T.sem["l_" + m], pid, rid, bits(engines(topo, y, d, m)))
+    for _, m, r in todo:
+        s, y, d = pl[(r, m)]
+        g.wait_ge(T.sem["l_" + m], len(engines(topo, y, d, m)))
+
+
+def rank_program(g, core, T, topo):
+    pl = plan(T, topo)
+    rank = T.rank_of(core)
+    if rank is None:
+        return relay_program(g, core, T, topo, pl)
+    Q = {"V": g.vector, "A": g.scalar, "P": g.tensor, "G": g, "S": g.sync}
+    cnt = {}
+    know = {e: {} for e in Q}
+    know["net"] = {}
+    hist = {}
+
+    def b(name, lo=0, hi=None, step=1, p=(0, 128)):
+        name, first, width = PLACE[name]
+        hi = first + (width if hi is None else hi)
+        lo += first
+        ap = T[name][p[0]:p[1], lo:hi] if step == 1 else T[name][p[0]:p[1], lo:hi:step]
+        return (ap, name, (0, 1, lo, hi))
+
+    def b3(name, c0, c1, lo, hi, p=(0, 128)):
+        return (T[name][p[0]:p[1], c0:c1, lo:hi], name, (c0, c1, lo, hi))
+
+    def b2(name, c, lo, hi, p=(0, 128)):
+        return (T[name][p[0]:p[1], c, lo:hi], name, (c, c + 1, lo, hi))
+
+    def ind(win, off):
+        return (win[0].indirect(off[0]), win[1], win[2], off)
+
+    def hits(x, y):
+        return x[0] < y[1] and y[0] < x[1] and x[2] < y[3] and y[2] < x[3]
+
+    def inside(x, y):
+        return x[0] >= y[0] and x[1] <= y[1] and x[2] >= y[2] and x[3] <= y[3]
+
+    def regions(ops):
+        return [(o[1], o[2], SCRATCH[o[1]][0] == "psum") for o in ops if isinstance(o, tuple)]
+
+    def offsets(ops):
+        return [o[3] for o in ops if isinstance(o, tuple) and len(o) > 3]
+
+    def sync(e, reads, writes):
+        deps = {}
+        for w, lst in ((False, reads), (True, writes)):
+            for name, reg, psum in lst:
+                for (r2, w2, e2, sem, count, snap) in hist.get(name, []):
+                    if not (psum and e2 != e):
+                        if not (w or w2) or not hits(reg, r2):
+                            continue
+                        if e2 == e and (e == "P" or not w2) and e in ENG:
+                            continue
+                    if deps.get(sem, (0, None))[0] < count:
+                        deps[sem] = (count, snap)
+        k = know[e]
+        for sem in sorted(deps, key=lambda x: -len(deps[x][1])):
+            count, snap = deps[sem]
+            if k.get(sem, 0) < count:
+                Q[e].wait_ge(T.sem[sem], count)
+                k[sem] = count
+                for s2, v in snap.items():
+                    if k.get(s2, 0) < v:
+                        k[s2] = v
+
+    def note(e, reads, writes, sem, n):
+        cnt[sem] = cnt.get(sem, 0) + n
+        snap = dict(know[e])
+        for w, lst in ((False, reads), (True, writes)):
+            for name, reg, psum in lst:
+                keep = [x for x in hist.get(name, [])
+                        if not (inside(x[0], reg) and (w or (not x[1] and x[2] == e and x[3] == sem)))]
+                hist[name] = keep + [(reg, w, e, sem, cnt[sem], snap)]
+
+    def op(e, f, out, ins):
+        reads, writes = regions(ins + offsets(ins + [out])), regions([out])
+        sync(e, reads, writes)
+        f(Q[e]).then_inc(T.sem["q" + e], 1)
+        note(e, reads, writes, "q" + e, 1)
+
+    def A_(o):
+        return o[0] if isinstance(o, tuple) else o
+
+    def tt(out, a, c, o):
+        op("V", lambda q: q.tensor_tensor(A_(out), A_(a), A_(c), o), out, [a, c])
+
+    def ts(out, a, s1, o1, s2=None, o2=None):
+        if o2 is None:
+            op("V", lambda q: q.tensor_scalar(A_(out), A_(a), A_(s1), None, o1), out, [a, s1])
+        else:
+            op("V", lambda q: q.tensor_scalar(A_(out), A_(a), A_(s1), A_(s2), o1, o2), out, [a, s1, s2])
+
+    def cp(out, a):
+        op("V", lambda q: q.tensor_copy(A_(out), A_(a)), out, [a])
+
+    def scan(out, d0, d1, o0, o1):
+        op("V", lambda q: q.tensor_tensor_scan(A_(out), A_(d0), A_(d1), 0.0, o0, o1), out, [d0, d1])
+
+    def ms(out, v):
+        op("V", lambda q: q.memset(A_(out), v), out, [])
+
+    def act(out, a, fn=AF.Copy, scale=1.0, bias=0.0):
+        op("A", lambda q: q.activation(A_(out), A_(a), fn, bias=A_(bias), scale=A_(scale)), out, [a, scale, bias])
+
+    tiles = {}
+
+    def mm(out, l, r, st, sp, tile=None):
+        was = tiles.get(out[1], (tile, 0))
+        if tile is not None and was[0] != tile and know["P"].get("qP", 0) < was[1]:
+            g.tensor.wait_ge(T.sem.qP, was[1])
+            know["P"]["qP"] = was[1]
+        op("P", lambda q: q.matmul(A_(out), A_(l), A_(r), st, sp), out, [l, r])
+        tiles[out[1]] = (tile, cnt["qP"])
+
+    def iota(out, pat, base, cm):
+        if SCRATCH[out[1]][2] == I32:
+            op("G", lambda q: q.iota(A_(out), pat, base, cm), out, [])
+        else:
+            op("G", lambda q: q.iota(A_(out), pat, base, cm, allow_small_or_imprecise_dtypes=True), out, [])
+
+    def asel(out, a, pat, o, base, cm):
+        op("G", lambda q: q.affine_select(A_(out), A_(a), pat, o, 0.0, base, cm), out, [a])
+
+    def scat(win, width, off, n, val):
+        cp(ind(b(win, 0, width), b(off, 0, n)), val)
+
+    def load(e, out, src, name):
+        w = regions([out])
+        sync(e, [], w)
+        Q[e].dma_start(out[0], src).then_inc(T.sem["d_" + name], 16)
+        note(e, [], w, "d_" + name, 16)
+
+    def store(e, dst, a, name):
+        r = regions([a])
+        sync(e, r, [])
+        Q[e].dma_start(dst, a[0]).then_inc(T.sem["o_" + name], 16)
+        note(e, r, [], "o_" + name, 16)
+
+    for (r_, m_), (s_, y_, d_) in pl.items():
+        if d_ == core:
+            note("net", [], regions([b(m_, 0, S) if m_ in TABLES else b(m_)]), "a_" + m_,
+                 len(engines(topo, s_ if y_ is None else y_, d_, m_)))
+
+    def send(m, src):
+        s, y, d = pl[(rank, m)]
+        to = d if y is None else y
+        r = regions([src])
+        sync("G", r, [])
+        es = engines(topo, core, to, m)
+        rid, pid = topo.addr(to, core)
+        g.remote_dma(land(T, m), src[0], T.sem["a_" + m], T.sem["l_" + m], pid, rid, bits(es))
+        note("G", r, [], "l_" + m, len(es))
+
+    load("S", b("EFI", 0, L), T.ef[:, 0:L], "ef0")
+    load("A", b("HT", 0, S), T.tab[:, :], "tab")
+    load("S", b("EHI", 0, L), T.eh[:, 0:L], "eh0")
+    load("S", b("ZF", 0, L), T.zf[:, 0:L], "zf0")
+    load("S", b("TC"), T.tab[:, :], "tc")
+    load("S", b("EFI", L, F), T.ef[:, L:F], "ef1")
+    load("S", b("EHI", L, F), T.eh[:, L:F], "eh1")
+    load("S", b("ZF", L, F), T.zf[:, L:F], "zf1")
+
+    ms(b("ONB"), 1.0)
+    iota(b("PI"), [[0, 1]], 0, 1)
+    iota(b("KIO"), [[0, 13], [1, 16]], 0, 0)
+    asel(b("BA"), b("ONB"), [[-16, 8], [0, 16]], OP.is_ge, 0, 1)
+    asel(b("BO"), b("BA"), [[16, 8], [0, 16]], OP.is_ge, 15, -1)
+    asel(b("ID"), b("ONB"), [[-1, 128]], OP.is_equal, 0, 1)
+    iota(b("EX0", 0, 13), [[16, 13]], 0, -1)
+    iota(b("EX1", 0, 13), [[16, 13]], -NB, -1)
+    ts(b("PJ"), b("PI"), 15, OP.bitwise_and)
+    ts(b("PK"), b("PI"), 4, OP.arith_shift_right, 1, OP.bitwise_and)
+    cp(b("PM"), b("PJ"))
+    cp(b("MH1"), b("PK"))
+    ts(b("MH0"), b("MH1"), -1.0, OP.mult, 1.0, OP.add)
+    ts(b("PW"), b("PM"), -1.0, OP.mult, 11.0, OP.add)
+    act(b("PW"), b("PW"), AF.Exp, LN2)
+    for x in (0, 1):
+        ex = "EX%d" % x
+        ts(b(ex, 0, 13), b(ex, 0, 13), 60.0, OP.min, -60.0, OP.max)
+        act(b("W%d" % x, 0, 13), b(ex, 0, 13), AF.Exp, LN2)
+    ts(b("THR"), b("PW"), 2.5 / 2048.0, OP.mult)
+    ms(b("MB", 0, 1), 200.0)
+    ms(b("MB", 1, 2), -10.0)
+    ms(b("WMU"), 0.0)
+    ts(b("WMU", 15, 143, 16), b("BO", 0, 128, 16), float(PEN), OP.mult)
+    ts(b("NBO"), b("BO"), -1.0, OP.mult)
+    ts(b("KAD"), b("KIO"), -2048.0, OP.mult, 30720.0, OP.add)
+    ts(b("RKM"), b("KIO"), 0.0, OP.is_gt)
+    ts(b("M16"), b("KIO"), b("PM"), OP.is_equal)
+
+    def pack(lo, hi):
+        ts(b("EE", lo, hi), b("EFI", lo, hi), 4096.0, OP.mult)
+        tt(b("EE", lo, hi), b("EE", lo, hi), b("EHI", lo, hi), OP.add)
+
+    def lists(x, c0, c1, t):
+        n0, n1 = 16 * c0, 16 * c1
+        ts(b3("I3", c0, c1, 0, 16), x, b("MH0"), OP.mult)
+        act(b3("I3", c0, c1, 16, 32), x, scale=b("MH1"))
+        y = b3("Y3", c0, c1, 0, 32)
+        op("V", lambda q: q.transpose(y[0], T.I3[:, c0:c1, :]), y, [b3("I3", c0, c1, 0, 32)])
+        tt(b3("XI", c0, c1, 0, 16), b3("Y3", c0, c1, 0, 16), b3("Y3", c0, c1, 16, 32), OP.add)
+        ts(b2("HF", 0, n0, n1), b3("XI", c0, c1, 0, 16), 2047, OP.bitwise_and)
+        ts(b2("HF", 1, n0, n1), b3("XI", c0, c1, 0, 16), 12, OP.arith_shift_right, 2047, OP.bitwise_and)
+        cp(b3("LI%d" % t, 0, 2, n0, n1), b3("HF", 0, 2, n0, n1))
+
+    def half(t, x):
+        return lambda lo, hi: b2("LI%d" % t, x, lo, hi)
+
+    def keyadd(c0, c1, t):
+        n0, n1 = 16 * c0, 16 * c1
+        tt(b("KA%d" % t, n0, n1), b("KAD", n0, n1), b2("HF", 0, n0, n1), OP.add)
+
+    def expand(z, src, c0, c1, cp=cp):
+        cp(b3(z, c0, c1, 0, 16), src)
+        for w in (16, 32, 64, 128):
+            cp(b3(z, c0, c1, w, 2 * w), b3(z, c0, c1, 0, w))
+
+    bank = [0]
+
+    def bulk(win, lst, z, cm, vch, ach):
+        pend = []
+
+        def sig():
+            c0, c1, t = pend.pop(0)
+            act(b(cm, 256 * c0, 256 * c1), b(t, 0, 256 * (c1 - c0)), AF.Sigmoid, 400.0, b("MB", 0, 1))
+        for c0, c1 in ach:
+            w = 256 * (c1 - c0)
+            ga, t = "GA%d" % (bank[0] % 3), "T%d" % (bank[0] % 6)
+            bank[0] += 1
+            act(b(ga, 0, w), ind(b(win, 0, S), lst(16 * c0, 16 * c1)), scale=-1.0)
+            mm(b(t, 0, w), b("ID"), b3(z, c0, c1, 0, 256), True, False)
+            mm(b(t, 0, w), b("ID"), b(ga, 0, w), False, True)
+            pend.append((c0, c1, t))
+            if len(pend) > 1:
+                sig()
+        while pend:
+            sig()
+        for c0, c1 in vch:
+            for c in range(c0, c1):
+                tt(b(cm, 256 * c, 256 * c + 256), ind(b(win, 0, S), lst(16 * c, 16 * c + 16)), b2(z, c, 0, 256), OP.is_le)
+
+    def psum(cm, dst, c0, c1):
+        for m in range(16):
+            mm(b(dst, 16 * c0, 16 * c1), b("WMU", 15 - m, 143 - m), b(cm, 256 * c0 + m, 256 * c1, 16), m == 0, m == 15)
+
+    def home_max(t):
+        tt(b("HK"), b("PH", 0, L), b("KA%d" % t), OP.add)
+        scan(b("HS"), b("RKM"), b("HK"), OP.mult, OP.max)
+        cp(b("HKI", 0, 13), b("HS", 15, L, 16))
+        ts(b("HSL", 0, 13), b("HKI", 0, 13), 2047, OP.bitwise_and)
+        ts(b("A1", 0, 13), b("HKI", 0, 13), float(9 * PEN), OP.is_ge, float(9 * PEN), OP.mult)
+        ts(b("AP", 0, 13), b("HSL", 0, 13), float(OKB), OP.add)
+        tt(b("AP", 0, 13), b("AP", 0, 13), b("A1", 0, 13), OP.max)
+
+    JOBS = []
+    for h in (0, 1):
+        for a in (h, 2 + h):
+            JOBS += [(2 * a, "T%d" % a, 0, 0), (2 * a + 1, "T%d" % a, L, 0)]
+        JOBS += [(2 * h + x, "T4", 192 * h + 96 * x, 1) for x in (0, 1)]
+        JOBS += [(4 + 2 * h + x, ("T5", "PF")[h], L * h + 96 * x, 1) for x in (0, 1)]
+
+    def decide(t, kf, idle=None):
+        tt(b("YY", 0, 13), b("AP", 0, 13), kf, OP.max)
+        ts(b("IX", 0, 13), b("YY", 0, 13), float(OKB + S), OP.min, float(OKB), OP.subtract)
+        act(b("B1"), ind(b("CT1", 0, S + 16), b("IX", 0, 13)))
+        cp(b("B0"), ind(b("CT0", 0, S + 16), b("IX", 0, 13)))
+        for gg, t_, o, blk in JOBS:
+            pp, lo, n = (32 * (gg // 2), 32 * (gg // 2) + 32), (0, NB)[blk], (NB, 96)[blk]
+            bb = "B%d" % (gg % 2)
+            mm(b(t_, o, o + L - lo, p=(0, n)), b(bb, lo, lo + n, p=pp), b(bb, lo, L, p=pp), True, True, gg // 2)
+        for gg, t_, o, blk in JOBS:
+            w, pp = (L, 96)[blk], (0, (NB, 96)[blk])
+            out = b3("E%d" % blk, 0, (13, 6)[blk], 16 * gg, 16 * gg + 16, p=pp)
+            if t_ in ("T2", "T3", "PF"):
+                act(out, b(t_, o, o + w, p=pp), AF.Relu, 1.0, b("MB", 1, 2, p=pp))
+            else:
+                ts(out, b(t_, o, o + w, p=pp), 10.5, OP.is_ge)
+        ts(b("D0", 0, 13), b("YY", 0, 13), float(-OKB), OP.add)
+        for c in range(13):
+            mm(b("PH", 416 + c, 417 + c), b2("E0", c, 0, 128, p=(0, NB)), b("W0", c, c + 1, p=(0, NB)), True, c < 7)
+            if c >= 7:
+                mm(b("PH", 416 + c, 417 + c), b2("E1", c - 7, 0, 128, p=(0, 96)), b("W1", c, c + 1, p=(0, 96)), False, True)
+        tt(b("WM", 0, 13), b("HS", 15, L, 16), kf, OP.max)
+        cp(b("WI", 0, 13), b("WM", 0, 13))
+        ts(b("WS", 0, 13), b("WI", 0, 13), 15, OP.arith_shift_right)
+        ts(b("WR", 0, 13), b("WS", 0, 13), 9.0, OP.is_ge)
+        tt(b("WV", 0, 13), b("WR", 0, 13), b("WS", 0, 13), OP.mult)
+        tt(b("XB"), ind(b("WV", 0, 16), b("BL", 0, 13)), b("M16"), OP.mult)
+        mm(b("PF", L, 2 * L), b("BO"), b("XB"), True, True)
+        if idle:
+            idle()
+        ts(b("L1", 0, 13), b("PH", 416, 429), b("THR"), OP.is_gt, 4096.0, OP.mult)
+        tt(b("D2", 0, 13), b("L1", 0, 13), b("D0", 0, 13), OP.max)
+        tt(b("DS%d" % t, 0, 13), b("D2", 0, 13), b("DU%d" % t, 0, 13), OP.min)
+        cp(b("DT%d" % t, 0, 13), b("DS%d" % t, 0, 13))
+
+    def ranks(n):
+        scan(b("UC", 0, n), b("ON32", 0, n), b("UU", 0, n), OP.mult, OP.add)
+        mm(b("PF", 416, 416 + n), b("BO"), b("UC", 0, n), True, False)
+        mm(b("PF", 416, 416 + n), b("NT"), b("UU", 0, n), False, True)
+        mm(b("PF", 448, 449), b("BO"), b("UC", n - 1, n), True, True)
+
+    def lanes(t, n, fill, val):
+        pls, lw, lu = "PL%d" % t, "LW%d" % t, "LU%d" % t
+        ts(b("TB"), b("PF", 448, 449), -1.0, OP.mult, float(fill), OP.add)
+        tt(b("QQ", 0, n), b("PF", 416, 416 + n), b("NU", 0, n), OP.max)
+        cp(b(pls, 0, n), b("QQ", 0, n))
+        act(b(lw, 80, 208), b("L128"), AF.Identity, 1.0, b("TB"))
+        cp(ind(b(lw, 80, 80 + 1024), b(pls, 0, n)), val)
+        tt(b("XM"), b(lw, 80, 208), b("M16", 0, 128), OP.mult)
+        scan(b("XS"), b("RKM", 0, 128), b("XM"), OP.mult, OP.add)
+        cp(b(lu, 0, 8), b("XS", 15, 128, 16))
+
+    AS, VS = [(0, 2), (2, 3)], [(3, 5)]
+    AD, VD = [(9, 11), (5, 6)], [(6, 9), (11, 13)]
+    A0, V0 = [(0, 2), (2, 3), (9, 11)], [(3, 9), (11, 13)]
+
+    def step(t, ftab, update, idle, idle2=None):
+        lu, hl, fl, z = "LU%d" % t, half(t, 0), half(t, 1), "Z16%d" % t
+        bulk("HT", hl, z, "CMH", VS, AS)
+        act(b("DQ"), ind(b("D"), b(lu, 0, 8)), scale=4097.0)
+        act(b("ZL%d" % t, 80, L), ind(b("ZF"), b(lu, 0, 8)))
+        tt(b("XE"), ind(b("EE"), b(lu, 0, 8)), b("DQ"), OP.add)
+        lists(b("XE"), 5, 13, t)
+        update()
+        bulk(ftab, fl, z, "CMF", VS, AS)
+        psum("CMH", "PH", 0, 5)
+        expand(z, b("ZL%d" % t, 80, L), 5, 13)
+        keyadd(5, 13, t)
+        bulk("HT", hl, z, "CMH", VD, AD)
+        psum("CMF", "PF", 0, 5)
+        bulk(ftab, fl, z, "CMF", VD, AD)
+        psum("CMH", "PH", 5, 13)
+        psum("CMF", "PF", 5, 9)
+        home_max(t)
+        psum("CMF", "PF", 9, 13)
+        idle()
+        scan(b("FS"), b("RKM"), b("PF", 0, L), OP.mult, OP.max)
+        decide(t, b("FS", 15, L, 16), idle2)
+
+    send("RQZ", b("ZF", 0, L))
+    send("U3Z", b("ZF", 0, L))
+    send("U2Z", b("ZF", 0, L))
+    pack(0, L)
+    lists(b("EE", 0, L), 0, 13, 0)
+    send("RQL", b2("LI0", 1, 0, L))
+    expand("Z160", b("ZF", 0, L), 0, 13)
+    keyadd(0, 13, 0)
+    send("F2", b("TC"))
+    send("F3", b("TC"))
+    asel(b("NT"), b("NBO"), [[-1, 128]], OP.is_ge, 0, 1)
+    iota(b("CL", 0, 256), [[1, 256]], 0, 0)
+    iota(b("CL", 256, 264), [[256, 8]], 0, 0)
+    iota(b("C16", 0, 26), [[16, 26]], 0, 0)
+    iota(b("BLF", 0, 13), [[1, 13]], 0, 0)
+    iota(b("F2V", 0, 80), [[1, 80]], 544, 0)
+    iota(b("F2V", 80, 416), [[1, 336]], 0, 0)
+    bulk("HT", half(0, 0), "Z160", "CMH", V0, A0)
+    expand("ZR", b("RQZ"), 0, 13)
+    bulk("HT", lambda lo, hi: b("RQL", lo, hi), "ZR", "CMF", V0, A0)
+    psum("CMH", "PH", 0, 13)
+    for c in (0, 5, 9):
+        psum("CMF", "PF", c, {0: 5, 5: 9, 9: 13}[c])
+    cp(b("PX"), b("PW"))
+    cp(b("PY"), b("PX"))
+    ts(b("CI"), b("CL"), b("PY"), OP.mult)
+    ts(b("CJ"), b("CI"), 2048, OP.bitwise_and)
+    ts(b("CB"), b("CJ"), 1.0 / 1024.0, OP.mult, -1.0, OP.add)
+    ts(b("ML", 2, 3), b("PM"), 8.0, OP.is_lt)
+    ts(b("MH", 2, 3), b("PM"), 11.0, OP.is_lt)
+    tt(b("MH", 2, 3), b("MH", 2, 3), b("ML", 2, 3), OP.subtract)
+    for x in (0, 1):
+        tt(b("ML", x, x + 1), b("ML", 2, 3), b("MH%d" % x), OP.mult)
+        tt(b("MH", x, x + 1), b("MH", 2, 3), b("MH%d" % x), OP.mult)
+        ts(b2("LB", x, 0, 256), b("CB", 0, 256), b("ML", x, x + 1), OP.mult)
+        ts(b2("HB", x, 0, 8), b("CB", 256, 264), b("MH", x, x + 1), OP.mult)
+        ms(b("CT%d" % x, S, S + 16), 0.0)
+    ms(b("KFO"), 0.0)
+    scan(b("FS"), b("RKM"), b("PF", 0, L), OP.mult, OP.max)
+    cp(b("KFO", 0, 13), b("FS", 15, L, 16))
+    send("KFR", b("KFO"))
+    home_max(0)
+    iota(b("LW1", 0, 80), [[1, 80]], 544, 0)
+    iota(b("LW2", 0, 80), [[1, 80]], 464, 0)
+    iota(b("L128"), [[1, 128]], 0, 0)
+    iota(b("OC"), [[0, WT]], -1, 0)
+    iota(b("LVF"), [[64, 2], [0, 512]], 0, 0)
+    iota(b("LVW"), [[0, 1024]], 0, 0)
+    for h in range(8):
+        act(b("CT1", 256 * h, 256 * h + 256), b2("LB", 1, 0, 256), AF.Identity, 1.0, b2("HB", 1, h, h + 1))
+        ts(b("CT0", 256 * h, 256 * h + 256), b2("LB", 0, 0, 256), b2("HB", 0, h, h + 1), OP.add)
+    ts(b("FW", 0, 26), b("C16", 0, 26), b("PM"), OP.add)
+    for t in range(3):
+        ts(b("DU%d" % t, 0, 13), b("FW", 0, 13), float(S + 256 * t), OP.add)
+    ts(b("DMF", 0, 26), b("FW", 0, 26), 512.0, OP.add)
+    cp(b("BL", 0, 13), b("BLF", 0, 13))
+    for n_, v_ in (("WV", 0.0), ("WN", 0.0), ("DT0", 0), ("DT1", 0), ("ON32", 1.0), ("D", 0.0), ("BP", 0.0)):
+        ms(b(n_), v_)
+
+    def known_z(t, f0):
+        act(b("ZL%d" % t, 0, 80), b("ZF", f0, f0 + 80))
+        expand("Z16%d" % t, b("ZF", f0, f0 + 80), 0, 5, act)
+    pack(L, F)
+    for t, f0 in ((1, 544), (2, 464)):
+        lists(b("EE", f0, f0 + 80), 0, 5, t)
+        keyadd(0, 5, t)
+    known_z(1, 544)
+    decide(0, b("KFR", 0, 13), lambda: known_z(2, 464))
+    send("U2D", b("DT0"))
+    send("U3D", b("DT0"))
+
+    ts(b("UU", 0, 13), b("DS0", 0, 13), float(S), OP.is_ge)
+    ranks(13)
+    ts(b("NU", 0, 13), b("DS0", 0, 13), float(S), OP.is_lt)
+    tt(b("NU", 0, 13), b("NU", 0, 13), b("DMF", 0, 13), OP.mult)
+    scat("HT", WT, "DT0", 13, b("ZF", 0, L))
+    lanes(1, 13, 208, b("F2V", 80, 288))
+    act(b("D", 0, L), b("PF", L, 2 * L))
+
+    def update1():
+        send("V3Z", b("ZL1"))
+        scat("F2", WT, "U2D", 13, b("U2Z"))
+    step(1, "F2", update1, lambda: scat("OC", WT, "DT0", 13, b("F2V", 80, 288)), lambda: scat("F3", WT, "U3D", 13, b("U3Z")))
+    send("V3D", b("DT1"))
+
+    ts(b("WN", 0, 13), b("DS1", 0, 13), float(S), OP.is_lt, 64.0, OP.mult)
+    tt(b("XB"), ind(b("WN", 0, 16), b("BL", 0, 13)), b("M16"), OP.mult)
+    mm(b("PH", L, 2 * L), b("BO"), b("XB"), True, True)
+    act(b("LVF", 0, 128), b("PH", L + 80, 2 * L))
+    act(b("LVW", 0, 128), b("PF", L + 80, 2 * L))
+    act(b("D", 544, F), b("PF", L, L + 80))
+    ts(b("TU"), b("TB"), -1.0, OP.mult)
+    ts(b("PL1", 13, 21), b("FW", 13, 21), b("TU"), OP.add)
+    scat("OC", WT, "DT1", 13, b("LW1", 0, L))
+    tt(b("BP", 0, L), ind(b("OC"), b("DT0", 0, 13)), b("F2V", 80, 288), OP.not_equal)
+    ts(b("UF"), ind(b("LVF"), b("PL1", 0, 21)), 64.0, OP.is_lt)
+    for x in ("BP", "UF"):
+        for m in range(16):
+            mm(b("PH", 450, 471), b("WMU", 15 - m, 143 - m), b(x, m, 336, 16), x == "BP" and m == 0, x == "UF" and m == 15)
+    ts(b("UU", 0, 5), b("DS1", 0, 5), float(S), OP.is_ge)
+    scat("HT", WT, "DT1", 13, b("ZL1"))
+    act(b("GW"), ind(b("LVW"), b("PL1", 0, 21)))
+    ts(b("UU", 5, 26), b("PH", 450, 471), 1.0, OP.is_ge)
+    ranks(26)
+    ts(b("NU", 0, 26), b("UU", 0, 26), -1.0, OP.mult, 1.0, OP.add)
+    tt(b("NU", 0, 26), b("NU", 0, 26), b("DMF", 0, 26), OP.mult)
+    lanes(2, 26, 336, b("F2V"))
+    for i, x in enumerate(("D", "GW", "BP")):
+        mm(b("T5", 0, 336), b("ID"), b(x, 0, 336), i == 0, i == 2)
+    act(b("D", 0, 336), b("T5", 0, 336))
+
+    def idle2():
+        ts(b("NB1"), b("BP", 0, L), -1.0, OP.mult, 1.0, OP.add)
+        act(b("DL"), ind(b("D"), b("LU2", 0, 8)))
+        ms(b("DF", 336, 464), 0.0)
+    step(2, "F3", lambda: scat("F3", WT, "V3D", 13, b("V3Z")), idle2)
+
+    scat("HT", WT, "DT2", 13, b("ZL2"))
+    store("S", T.yt[:, :], b("HT", 0, S), "yt")
+    scat("OC", WT, "DT2", 13, b("LW2", 0, L))
+    store("A", T.yo[:, :], (T.OC[0:128:16, 0:S], "OC", (0, 1, 0, S)), "yo")
+    tt(b("B3"), ind(b("OC"), b("DT0", 0, 13)), b("F2V", 80, 288), OP.not_equal)
+    tt(b("HK"), ind(b("OC"), b("DT1", 0, 13)), b("LW1", 0, L), OP.not_equal)
+    tt(b("BP", 0, L), b("B3"), b("NB1"), OP.mult)
+    cp(b("LVW", 0, 128), b("HK", 80, L))
+    cp(b("B2"), ind(b("LVW"), b("PL1", 0, 21)))
+    for i, x in enumerate(("D", "BP", "B2")):
+        mm(b("T4", 0, 336), b("ID"), b(x, 0, 336), i == 0, i == 2)
+    tt(b("ND"), b("DL"), b("PF", L + 80, 2 * L), OP.add)
+    cp(b("DF", 464, 544), b("PF", L, L + 80))
+    tt(b("DF", 544, F), b("D", 544, F), b("HK", 0, 80), OP.add)
+    cp(b("DF", 0, 336), b("T4", 0, 336))
+    scat("DF", F, "LU2", 8, b("ND"))
+    store("S", T.yd[:, :], (T.DF[0:128:16, 0:F], "DF", (0, 1, 0, F)), "yd")
+    for s in SEMAPHORES:
+        if s in cnt and know["G"].get(s, 0) < cnt[s]:
+            g.wait_ge(T.sem[s], cnt[s])

@@ -9,6 +9,7 @@ PEN = 32768
 OKB = 8 * PEN
 NB = 112
 LN2 = math.log(2.0)
+LAG, SLACK = 0.1, 0.05
 
 ENG = "VAPG"
 LOADS = ["ef0", "eh0", "zf0", "tab", "tc", "ef1", "eh1", "zf1"]
@@ -131,16 +132,16 @@ def rank_program(g, core, T, topo):
         hi = first + (width if hi is None else hi)
         lo += first
         ap = T[name][p[0]:p[1], lo:hi] if step == 1 else T[name][p[0]:p[1], lo:hi:step]
-        return (ap, name, (0, 1, lo, hi))
+        return (ap, name, (0, 1, lo, hi), None, -(-(hi - lo) // step))
 
     def b3(name, c0, c1, lo, hi, p=(0, 128)):
-        return (T[name][p[0]:p[1], c0:c1, lo:hi], name, (c0, c1, lo, hi))
+        return (T[name][p[0]:p[1], c0:c1, lo:hi], name, (c0, c1, lo, hi), None, (c1 - c0) * (hi - lo))
 
     def b2(name, c, lo, hi, p=(0, 128)):
-        return (T[name][p[0]:p[1], c, lo:hi], name, (c, c + 1, lo, hi))
+        return (T[name][p[0]:p[1], c, lo:hi], name, (c, c + 1, lo, hi), None, hi - lo)
 
     def ind(win, off):
-        return (win[0].indirect(off[0]), win[1], win[2], off)
+        return (win[0].indirect(off[0]), win[1], win[2], off, 16 * off[4])
 
     def hits(x, y):
         return x[0] < y[1] and y[0] < x[1] and x[2] < y[3] and y[2] < x[3]
@@ -152,7 +153,7 @@ def rank_program(g, core, T, topo):
         return [(o[1], o[2], SCRATCH[o[1]][0] == "psum") for o in ops if isinstance(o, tuple)]
 
     def offsets(ops):
-        return [o[3] for o in ops if isinstance(o, tuple) and len(o) > 3]
+        return [o[3] for o in ops if isinstance(o, tuple) and o[3]]
 
     def sync(e, reads, writes):
         deps = {}
@@ -185,11 +186,74 @@ def rank_program(g, core, T, topo):
                         if not (inside(x[0], reg) and (w or (not x[1] and x[2] == e and x[3] == sem)))]
                 hist[name] = keep + [(reg, w, e, sem, cnt[sem], snap)]
 
-    def op(e, f, out, ins):
+    def emit(e, f, out, ins):
         reads, writes = regions(ins + offsets(ins + [out])), regions([out])
         sync(e, reads, writes)
         f(Q[e]).then_inc(T.sem["q" + e], 1)
         note(e, reads, writes, "q" + e, 1)
+
+    nodes, seen, group = [], {}, []
+
+    def node(e, run, reads, writes, dur, lat=0.0, after=None):
+        k, before = len(nodes), {}
+        if after is not None:
+            before[after] = 1
+        for w, lst in ((False, reads), (True, writes)):
+            for name, reg, psum in lst:
+                for (r2, w2, j) in seen.get(name, []):
+                    if nodes[j][0] == e == "P" and psum:
+                        if hits(reg, r2):
+                            before.setdefault(j, 0)
+                    elif (psum and nodes[j][0] != e) or ((w or w2) and hits(reg, r2)):
+                        before[j] = max(before.get(j, 0), 1 if w2 or nodes[j][0] != e else 0)
+        for w, lst in ((False, reads), (True, writes)):
+            for name, reg, psum in lst:
+                keep = [x for x in seen.get(name, []) if not (w and inside(x[0], reg) and not psum)]
+                seen[name] = keep + [(reg, w, k)]
+        nodes.append((e, run, dur, lat, sorted(before.items())))
+        return k
+
+    def op(e, f, out, ins, after=None):
+        win = [x for x in ins if isinstance(x, tuple) and x[3]]
+        c = 0.00083 * max(x[4] for x in ins + [out] if isinstance(x, tuple))
+        if e == "G":
+            dur = 0.15 + 2 * c
+        elif out[3]:
+            dur = 0.05 + 3.5 * c
+        elif win:
+            dur = 0.06 + 1.56 * 0.00083 * out[4]
+        else:
+            two = all(SCRATCH[x[1]][2] in (BF, U16) for x in ins + [out] if isinstance(x, tuple))
+            both = len(ins) == 2 and all(isinstance(x, tuple) and x[4] == out[4] and SCRATCH[x[1]][0] == "sbuf" for x in ins)
+            dur = max(0.06, 0.05 + c * (0.5 if two else 2 if both else 1)) + (0.14 if e == "A" else 0)
+        node(e, lambda: emit(e, f, out, ins), regions(ins + offsets(ins + [out])), regions([out]), dur, 0.0, after)
+
+    def issue():
+        tail, left, free, end, succ = [0.0] * len(nodes), [len(x[4]) for x in nodes], {}, {}, [[] for _ in nodes]
+        for k, x in enumerate(nodes):
+            for j, full in x[4]:
+                succ[j].append((k, full))
+        for k in reversed(range(len(nodes))):
+            tail[k] = nodes[k][2] + max([0.0] + [tail[s] + (nodes[k][3] + LAG) * full for s, full in succ[k]])
+        ready, order = [k for k in range(len(nodes)) if not left[k]], []
+        while ready:
+            start, first = {}, {}
+            for k in ready:
+                e, run, dur, lat, before = nodes[k]
+                start[k] = max([free.get(e, 0.0)] + [end[j] - (0 if full else nodes[j][3]) + LAG * full for j, full in before])
+                first[e] = min(first.get(e, 1e9), start[k])
+            e = min(first, key=lambda x: first[x])
+            k = max((k for k in ready if nodes[k][0] == e and start[k] <= first[e] + SLACK), key=lambda k: (tail[k], -k))
+            ready.remove(k)
+            order.append(k)
+            free[e] = start[k] + nodes[k][2]
+            end[k] = free[e] + nodes[k][3]
+            for s, full in succ[k]:
+                left[s] -= 1
+                if not left[s]:
+                    ready.append(s)
+        for k in order:
+            nodes[k][1]()
 
     def A_(o):
         return o[0] if isinstance(o, tuple) else o
@@ -217,19 +281,30 @@ def rank_program(g, core, T, topo):
 
     tiles = {}
 
-    def mm(out, l, r, st, sp, tile=None):
+    def mm_now(out, l, r, st, sp, tile):
         was = tiles.get(out[1], (tile, 0))
         if tile is not None and was[0] != tile and know["P"].get("qP", 0) < was[1]:
             g.tensor.wait_ge(T.sem.qP, was[1])
             know["P"]["qP"] = was[1]
-        op("P", lambda q: q.matmul(A_(out), A_(l), A_(r), st, sp), out, [l, r])
+        emit("P", lambda q: q.matmul(A_(out), A_(l), A_(r), st, sp), out, [l, r])
         tiles[out[1]] = (tile, cnt["qP"])
 
-    def iota(out, pat, base, cm):
+    def mm(out, l, r, st, sp, tile=None):
+        group.append((out, l, r, st, sp, tile))
+        if sp and not group[0][0] == "open":
+            close()
+
+    def close():
+        m = [x for x in group if x[0] != "open"]
+        group.clear()
+        node("P", lambda: [mm_now(*x) for x in m], regions([x[1] for x in m] + [x[2] for x in m]), regions([x[0] for x in m]),
+             sum(0.02 + 0.00042 * max(64, x[0][4]) for x in m))
+
+    def iota(out, pat, base, cm, after=None):
         if SCRATCH[out[1]][2] == I32:
-            op("G", lambda q: q.iota(A_(out), pat, base, cm), out, [])
+            op("G", lambda q: q.iota(A_(out), pat, base, cm), out, [], after)
         else:
-            op("G", lambda q: q.iota(A_(out), pat, base, cm, allow_small_or_imprecise_dtypes=True), out, [])
+            op("G", lambda q: q.iota(A_(out), pat, base, cm, allow_small_or_imprecise_dtypes=True), out, [], after)
 
     def asel(out, a, pat, o, base, cm):
         op("G", lambda q: q.affine_select(A_(out), A_(a), pat, o, 0.0, base, cm), out, [a])
@@ -239,30 +314,41 @@ def rank_program(g, core, T, topo):
 
     def load(e, out, src, name):
         w = regions([out])
-        sync(e, [], w)
-        Q[e].dma_start(out[0], src).then_inc(T.sem["d_" + name], 16)
-        note(e, [], w, "d_" + name, 16)
+
+        def run():
+            sync(e, [], w)
+            Q[e].dma_start(out[0], src).then_inc(T.sem["d_" + name], 16)
+            note(e, [], w, "d_" + name, 16)
+        node(e, run, [], w, 0.1, 3.4 if out[4] > 700 else 2.4)
 
     def store(e, dst, a, name):
         r = regions([a])
-        sync(e, r, [])
-        Q[e].dma_start(dst, a[0]).then_inc(T.sem["o_" + name], 16)
-        note(e, r, [], "o_" + name, 16)
 
-    for (r_, m_), (s_, y_, d_) in pl.items():
-        if d_ == core:
-            note("net", [], regions([b(m_, 0, S) if m_ in TABLES else b(m_)]), "a_" + m_,
-                 len(engines(topo, s_ if y_ is None else y_, d_, m_)))
+        def run():
+            sync(e, r, [])
+            Q[e].dma_start(dst, a[0]).then_inc(T.sem["o_" + name], 16)
+            note(e, r, [], "o_" + name, 16)
+        node(e, run, r, [], 0.1, 5.0 if name == "yt" else 2.0)
 
     def send(m, src):
         s, y, d = pl[(rank, m)]
         to = d if y is None else y
         r = regions([src])
-        sync("G", r, [])
         es = engines(topo, core, to, m)
         rid, pid = topo.addr(to, core)
-        g.remote_dma(land(T, m), src[0], T.sem["a_" + m], T.sem["l_" + m], pid, rid, bits(es))
-        note("G", r, [], "l_" + m, len(es))
+
+        def run():
+            sync("G", r, [])
+            g.remote_dma(land(T, m), src[0], T.sem["a_" + m], T.sem["l_" + m], pid, rid, bits(es))
+            note("G", r, [], "l_" + m, len(es))
+        k = node("G", run, r, [], 0.1)
+        for (r_, m_), (s_, y_, d_) in pl.items():
+            if d_ == core and m_ == m:
+                w = regions([b(m, 0, S) if m in TABLES else b(m)])
+                n = len(engines(topo, s_ if y_ is None else y_, d_, m))
+                lat = (1.7 + (9.0 if m in TABLES else 0.8 if src[4] > 100 else 0.0)) * (1 if y_ is None else 2)
+                node("n" + m, lambda: note("net", [], w, "a_" + m, n), [], w, 0.0, lat, k)
+        return k
 
     load("S", b("EFI", 0, L), T.ef[:, 0:L], "ef0")
     load("A", b("HT", 0, S), T.tab[:, :], "tab")
@@ -310,8 +396,8 @@ def rank_program(g, core, T, topo):
         n0, n1 = 16 * c0, 16 * c1
         ts(b3("I3", c0, c1, 0, 16), x, b("MH0"), OP.mult)
         act(b3("I3", c0, c1, 16, 32), x, scale=b("MH1"))
-        y = b3("Y3", c0, c1, 0, 32)
-        op("V", lambda q: q.transpose(y[0], T.I3[:, c0:c1, :]), y, [b3("I3", c0, c1, 0, 32)])
+        y, i3 = b3("Y3", c0, c1, 0, 32), b3("I3", c0, c1, 0, 32)
+        op("V", lambda q: q.transpose(T.Y3[:, c0:c1, :], T.I3[:, c0:c1, :]), y, [i3])
         tt(b3("XI", c0, c1, 0, 16), b3("Y3", c0, c1, 0, 16), b3("Y3", c0, c1, 16, 32), OP.add)
         ts(b2("HF", 0, n0, n1), b3("XI", c0, c1, 0, 16), 2047, OP.bitwise_and)
         ts(b2("HF", 1, n0, n1), b3("XI", c0, c1, 0, 16), 12, OP.arith_shift_right, 2047, OP.bitwise_and)
@@ -332,11 +418,6 @@ def rank_program(g, core, T, topo):
     bank = [0]
 
     def bulk(win, lst, z, cm, vch, ach):
-        pend = []
-
-        def sig():
-            c0, c1, t = pend.pop(0)
-            act(b(cm, 256 * c0, 256 * c1), b(t, 0, 256 * (c1 - c0)), AF.Sigmoid, 400.0, b("MB", 0, 1))
         for c0, c1 in ach:
             w = 256 * (c1 - c0)
             ga, t = "GA%d" % (bank[0] % 3), "T%d" % (bank[0] % 6)
@@ -344,18 +425,15 @@ def rank_program(g, core, T, topo):
             act(b(ga, 0, w), ind(b(win, 0, S), lst(16 * c0, 16 * c1)), scale=-1.0)
             mm(b(t, 0, w), b("ID"), b3(z, c0, c1, 0, 256), True, False)
             mm(b(t, 0, w), b("ID"), b(ga, 0, w), False, True)
-            pend.append((c0, c1, t))
-            if len(pend) > 1:
-                sig()
-        while pend:
-            sig()
+            act(b(cm, 256 * c0, 256 * c1), b(t, 0, w), AF.Sigmoid, 400.0, b("MB", 0, 1))
         for c0, c1 in vch:
             for c in range(c0, c1):
                 tt(b(cm, 256 * c, 256 * c + 256), ind(b(win, 0, S), lst(16 * c, 16 * c + 16)), b2(z, c, 0, 256), OP.is_le)
 
-    def psum(cm, dst, c0, c1):
-        for m in range(16):
-            mm(b(dst, 16 * c0, 16 * c1), b("WMU", 15 - m, 143 - m), b(cm, 256 * c0 + m, 256 * c1, 16), m == 0, m == 15)
+    def psum(cm, dst, *cuts):
+        for c0, c1 in zip(cuts, cuts[1:]):
+            for m in range(16):
+                mm(b(dst, 16 * c0, 16 * c1), b("WMU", 15 - m, 143 - m), b(cm, 256 * c0 + m, 256 * c1, 16), m == 0, m == 15)
 
     def home_max(t):
         tt(b("HK"), b("PH", 0, L), b("KA%d" % t), OP.add)
@@ -373,7 +451,7 @@ def rank_program(g, core, T, topo):
         JOBS += [(2 * h + x, "T4", 192 * h + 96 * x, 1) for x in (0, 1)]
         JOBS += [(4 + 2 * h + x, ("T5", "PF")[h], L * h + 96 * x, 1) for x in (0, 1)]
 
-    def decide(t, kf, idle=None):
+    def decide(t, kf):
         tt(b("YY", 0, 13), b("AP", 0, 13), kf, OP.max)
         ts(b("IX", 0, 13), b("YY", 0, 13), float(OKB + S), OP.min, float(OKB), OP.subtract)
         act(b("B1"), ind(b("CT1", 0, S + 16), b("IX", 0, 13)))
@@ -390,10 +468,12 @@ def rank_program(g, core, T, topo):
             else:
                 ts(out, b(t_, o, o + w, p=pp), 10.5, OP.is_ge)
         ts(b("D0", 0, 13), b("YY", 0, 13), float(-OKB), OP.add)
+        group.append(("open",))
         for c in range(13):
             mm(b("PH", 416 + c, 417 + c), b2("E0", c, 0, 128, p=(0, NB)), b("W0", c, c + 1, p=(0, NB)), True, c < 7)
             if c >= 7:
                 mm(b("PH", 416 + c, 417 + c), b2("E1", c - 7, 0, 128, p=(0, 96)), b("W1", c, c + 1, p=(0, 96)), False, True)
+        close()
         tt(b("WM", 0, 13), b("HS", 15, L, 16), kf, OP.max)
         cp(b("WI", 0, 13), b("WM", 0, 13))
         ts(b("WS", 0, 13), b("WI", 0, 13), 15, OP.arith_shift_right)
@@ -401,8 +481,6 @@ def rank_program(g, core, T, topo):
         tt(b("WV", 0, 13), b("WR", 0, 13), b("WS", 0, 13), OP.mult)
         tt(b("XB"), ind(b("WV", 0, 16), b("BL", 0, 13)), b("M16"), OP.mult)
         mm(b("PF", L, 2 * L), b("BO"), b("XB"), True, True)
-        if idle:
-            idle()
         ts(b("L1", 0, 13), b("PH", 416, 429), b("THR"), OP.is_gt, 4096.0, OP.mult)
         tt(b("D2", 0, 13), b("L1", 0, 13), b("D0", 0, 13), OP.max)
         tt(b("DS%d" % t, 0, 13), b("D2", 0, 13), b("DU%d" % t, 0, 13), OP.min)
@@ -410,9 +488,11 @@ def rank_program(g, core, T, topo):
 
     def ranks(n):
         scan(b("UC", 0, n), b("ON32", 0, n), b("UU", 0, n), OP.mult, OP.add)
+        group.append(("open",))
         mm(b("PF", 416, 416 + n), b("BO"), b("UC", 0, n), True, False)
         mm(b("PF", 416, 416 + n), b("NT"), b("UU", 0, n), False, True)
         mm(b("PF", 448, 449), b("BO"), b("UC", n - 1, n), True, True)
+        close()
 
     def lanes(t, n, fill, val):
         pls, lw, lu = "PL%d" % t, "LW%d" % t, "LU%d" % t
@@ -429,7 +509,7 @@ def rank_program(g, core, T, topo):
     AD, VD = [(9, 11), (5, 6)], [(6, 9), (11, 13)]
     A0, V0 = [(0, 2), (2, 3), (9, 11)], [(3, 9), (11, 13)]
 
-    def step(t, ftab, update, idle, idle2=None):
+    def step(t, ftab, update, later):
         lu, hl, fl, z = "LU%d" % t, half(t, 0), half(t, 1), "Z16%d" % t
         bulk("HT", hl, z, "CMH", VS, AS)
         act(b("DQ"), ind(b("D"), b(lu, 0, 8)), scale=4097.0)
@@ -444,20 +524,20 @@ def rank_program(g, core, T, topo):
         bulk("HT", hl, z, "CMH", VD, AD)
         psum("CMF", "PF", 0, 5)
         bulk(ftab, fl, z, "CMF", VD, AD)
-        psum("CMH", "PH", 5, 13)
+        psum("CMH", "PH", 5, 9, 13)
         psum("CMF", "PF", 5, 9)
         home_max(t)
         psum("CMF", "PF", 9, 13)
-        idle()
+        later()
         scan(b("FS"), b("RKM"), b("PF", 0, L), OP.mult, OP.max)
-        decide(t, b("FS", 15, L, 16), idle2)
+        decide(t, b("FS", 15, L, 16))
 
     send("RQZ", b("ZF", 0, L))
     send("U3Z", b("ZF", 0, L))
     send("U2Z", b("ZF", 0, L))
     pack(0, L)
     lists(b("EE", 0, L), 0, 13, 0)
-    send("RQL", b2("LI0", 1, 0, L))
+    asked = send("RQL", b2("LI0", 1, 0, L))
     expand("Z160", b("ZF", 0, L), 0, 13)
     keyadd(0, 13, 0)
     send("F2", b("TC"))
@@ -468,13 +548,12 @@ def rank_program(g, core, T, topo):
     iota(b("C16", 0, 26), [[16, 26]], 0, 0)
     iota(b("BLF", 0, 13), [[1, 13]], 0, 0)
     iota(b("F2V", 0, 80), [[1, 80]], 544, 0)
-    iota(b("F2V", 80, 416), [[1, 336]], 0, 0)
+    iota(b("F2V", 80, 416), [[1, 336]], 0, 0, asked)
     bulk("HT", half(0, 0), "Z160", "CMH", V0, A0)
     expand("ZR", b("RQZ"), 0, 13)
     bulk("HT", lambda lo, hi: b("RQL", lo, hi), "ZR", "CMF", V0, A0)
-    psum("CMH", "PH", 0, 13)
-    for c in (0, 5, 9):
-        psum("CMF", "PF", c, {0: 5, 5: 9, 9: 13}[c])
+    psum("CMH", "PH", 0, 5, 9, 13)
+    psum("CMF", "PF", 0, 5, 9, 13)
     cp(b("PX"), b("PW"))
     cp(b("PY"), b("PX"))
     ts(b("CI"), b("CL"), b("PY"), OP.mult)
@@ -492,14 +571,16 @@ def rank_program(g, core, T, topo):
     ms(b("KFO"), 0.0)
     scan(b("FS"), b("RKM"), b("PF", 0, L), OP.mult, OP.max)
     cp(b("KFO", 0, 13), b("FS", 15, L, 16))
-    send("KFR", b("KFO"))
+    told = send("KFR", b("KFO"))
     home_max(0)
-    iota(b("LW1", 0, 80), [[1, 80]], 544, 0)
-    iota(b("LW2", 0, 80), [[1, 80]], 464, 0)
+    iota(b("LW1", 0, 80), [[1, 80]], 544, 0, told)
+    iota(b("LW2", 0, 80), [[1, 80]], 464, 0, told)
     iota(b("L128"), [[1, 128]], 0, 0)
-    iota(b("OC"), [[0, WT]], -1, 0)
-    iota(b("LVF"), [[64, 2], [0, 512]], 0, 0)
-    iota(b("LVW"), [[0, 1024]], 0, 0)
+    for x in range(0, WT, 704):
+        iota(b("OC", x, x + 704), [[0, 704]], -1, 0, told)
+    for x in (0, 512):
+        iota(b("LVF", x, x + 512), [[0, 512]], x // 8, 0, told)
+        iota(b("LVW", x, x + 512), [[0, 512]], 0, 0, told)
     for h in range(8):
         act(b("CT1", 256 * h, 256 * h + 256), b2("LB", 1, 0, 256), AF.Identity, 1.0, b2("HB", 1, h, h + 1))
         ts(b("CT0", 256 * h, 256 * h + 256), b2("LB", 0, 0, 256), b2("HB", 0, h, h + 1), OP.add)
@@ -510,16 +591,13 @@ def rank_program(g, core, T, topo):
     cp(b("BL", 0, 13), b("BLF", 0, 13))
     for n_, v_ in (("WV", 0.0), ("WN", 0.0), ("DT0", 0), ("DT1", 0), ("ON32", 1.0), ("D", 0.0), ("BP", 0.0)):
         ms(b(n_), v_)
-
-    def known_z(t, f0):
-        act(b("ZL%d" % t, 0, 80), b("ZF", f0, f0 + 80))
-        expand("Z16%d" % t, b("ZF", f0, f0 + 80), 0, 5, act)
     pack(L, F)
     for t, f0 in ((1, 544), (2, 464)):
         lists(b("EE", f0, f0 + 80), 0, 5, t)
         keyadd(0, 5, t)
-    known_z(1, 544)
-    decide(0, b("KFR", 0, 13), lambda: known_z(2, 464))
+        act(b("ZL%d" % t, 0, 80), b("ZF", f0, f0 + 80))
+        expand("Z16%d" % t, b("ZF", f0, f0 + 80), 0, 5, act)
+    decide(0, b("KFR", 0, 13))
     send("U2D", b("DT0"))
     send("U3D", b("DT0"))
 
@@ -534,7 +612,11 @@ def rank_program(g, core, T, topo):
     def update1():
         send("V3Z", b("ZL1"))
         scat("F2", WT, "U2D", 13, b("U2Z"))
-    step(1, "F2", update1, lambda: scat("OC", WT, "DT0", 13, b("F2V", 80, 288)), lambda: scat("F3", WT, "U3D", 13, b("U3Z")))
+
+    def later1():
+        scat("OC", WT, "DT0", 13, b("F2V", 80, 288))
+        scat("F3", WT, "U3D", 13, b("U3Z"))
+    step(1, "F2", update1, later1)
     send("V3D", b("DT1"))
 
     ts(b("WN", 0, 13), b("DS1", 0, 13), float(S), OP.is_lt, 64.0, OP.mult)
@@ -563,16 +645,16 @@ def rank_program(g, core, T, topo):
         mm(b("T5", 0, 336), b("ID"), b(x, 0, 336), i == 0, i == 2)
     act(b("D", 0, 336), b("T5", 0, 336))
 
-    def idle2():
+    def later2():
         ts(b("NB1"), b("BP", 0, L), -1.0, OP.mult, 1.0, OP.add)
         act(b("DL"), ind(b("D"), b("LU2", 0, 8)))
         ms(b("DF", 336, 464), 0.0)
-    step(2, "F3", lambda: scat("F3", WT, "V3D", 13, b("V3Z")), idle2)
+    step(2, "F3", lambda: scat("F3", WT, "V3D", 13, b("V3Z")), later2)
 
     scat("HT", WT, "DT2", 13, b("ZL2"))
     store("S", T.yt[:, :], b("HT", 0, S), "yt")
     scat("OC", WT, "DT2", 13, b("LW2", 0, L))
-    store("A", T.yo[:, :], (T.OC[0:128:16, 0:S], "OC", (0, 1, 0, S)), "yo")
+    store("A", T.yo[:, :], (T.OC[0:128:16, 0:S], "OC", (0, 1, 0, S), None, S), "yo")
     tt(b("B3"), ind(b("OC"), b("DT0", 0, 13)), b("F2V", 80, 288), OP.not_equal)
     tt(b("HK"), ind(b("OC"), b("DT1", 0, 13)), b("LW1", 0, L), OP.not_equal)
     tt(b("BP", 0, L), b("B3"), b("NB1"), OP.mult)
@@ -585,7 +667,8 @@ def rank_program(g, core, T, topo):
     tt(b("DF", 544, F), b("D", 544, F), b("HK", 0, 80), OP.add)
     cp(b("DF", 0, 336), b("T4", 0, 336))
     scat("DF", F, "LU2", 8, b("ND"))
-    store("S", T.yd[:, :], (T.DF[0:128:16, 0:F], "DF", (0, 1, 0, F)), "yd")
+    store("S", T.yd[:, :], (T.DF[0:128:16, 0:F], "DF", (0, 1, 0, F), None, F), "yd")
+    issue()
     for s in SEMAPHORES:
         if s in cnt and know["G"].get(s, 0) < cnt[s]:
             g.wait_ge(T.sem[s], cnt[s])

import math
from concourse.mybir import AluOpType, ActivationFunctionType
OP = AluOpType
AF = ActivationFunctionType
F32, BF, I32, U16 = "float32", "bfloat16", "int32", "uint16"
F, L, S = 624, 208, 2048
WT = S + 3 * 256
PEN = 32768
OKB = 8 * PEN
NB = 112
LN2 = math.log(2.0)
LAG, SLACK = 0.1, 0.05

ENG = "VAPG"
LOADS = ["ef0", "eh0", "zf0", "tab", "tc", "ef1", "eh1", "zf1"]
MSGS = ["RQZ", "RQL", "KFR", "F2", "F3", "U2Z", "U2D", "U3Z", "U3D", "V3Z", "V3D"]
TO = {"RQZ": 1, "RQL": 1, "KFR": -1, "F2": -2, "U2Z": -2, "U2D": -2, "F3": -3, "U3Z": -3, "U3D": -3, "V3Z": -3, "V3D": -3}
ORDER = ["RQZ", "U3Z", "RQL", "F3", "KFR", "U3D", "V3Z", "V3D"]
TABLES = ("F2", "F3")
STORES = ["yt", "yo", "yd"]
SEMAPHORES = (["q" + e for e in ENG] + ["d_" + n for n in LOADS] + ["o_" + n for n in STORES]
              + ["a_" + n for n in MSGS] + ["l_" + n for n in MSGS])

SCRATCH = {}
PLACE = {}
_fill = {F32: 0, BF: 0, I32: 0, U16: 0}


def _sb(name, shape, dtype):
    if len(shape) == 1 and shape[0] <= 48 and name not in MSGS + ["KFO", "DT0", "DT1"]:
        PLACE[name] = ("S" + dtype, _fill[dtype], shape[0])
        _fill[dtype] += -(-shape[0] // 16) * 16
        return
    SCRATCH[name] = ("sbuf", [128] + shape, dtype)
    PLACE[name] = (name, 0, shape[0])


for _n, _s, _d in (
        ("HT", [WT], BF), ("F2", [WT], BF), ("F3", [WT], BF), ("TC", [S], BF), ("OC", [WT], F32),
        ("ZF", [F], BF), ("EHI", [F], I32), ("EFI", [F], I32), ("EE", [F], F32), ("D", [F], BF), ("DF", [F], F32),
        ("XE", [128], F32), ("DQ", [128], F32), ("I3", [13, 32], F32), ("Y3", [13, 32], F32), ("XI", [13, 16], I32),
        ("HF", [2, L], I32), ("GA0", [512], BF), ("GA1", [512], BF), ("GA2", [512], BF),
        ("CMH", [3328], BF), ("CMF", [3328], BF), ("ZR", [13, 256], BF),
        ("RQZ", [L], BF), ("RQL", [L], U16), ("KFR", [16], F32), ("KFO", [16], F32),
        ("U2Z", [L], BF), ("U2D", [16], U16), ("U3Z", [L], BF), ("U3D", [16], U16), ("V3Z", [L], BF), ("V3D", [16], U16),
        ("HK", [L], F32), ("HS", [L], F32), ("FS", [L], F32), ("HKI", [16], I32), ("HSL", [16], I32), ("A1", [16], F32),
        ("AP", [16], F32), ("YY", [16], F32), ("IX", [16], U16), ("D0", [16], F32), ("L1", [16], F32), ("D2", [16], F32),
        ("WM", [16], F32), ("WI", [16], I32), ("WS", [16], I32), ("WR", [16], F32), ("WV", [16], F32), ("WN", [16], F32),
        ("XB", [L], BF), ("B0", [L], BF), ("B1", [L], BF), ("E0", [13, 128], BF), ("E1", [6, 128], BF),
        ("NU", [32], F32), ("UU", [32], BF), ("UC", [32], BF), ("QQ", [32], F32), ("TB", [1], F32), ("TU", [1], F32),
        ("XM", [128], F32), ("XS", [128], F32), ("LVF", [1024], F32), ("LVW", [1024], F32), ("UF", [336], BF),
        ("GW", [336], BF), ("BP", [336], BF), ("NB1", [L], F32), ("B2", [336], BF), ("B3", [L], F32), ("DL", [128], F32),
        ("ND", [128], F32),
        ("PI", [1], I32), ("PJ", [1], I32), ("PK", [1], I32), ("PM", [1], F32), ("MH0", [1], F32), ("MH1", [1], F32),
        ("PW", [1], F32), ("PX", [1], I32), ("PY", [1], F32), ("ML", [4], F32), ("MH", [4], F32), ("MB", [2], F32),
        ("KIO", [L], F32), ("M16", [L], F32), ("RKM", [L], F32), ("KAD", [L], F32), ("C16", [32], F32), ("FW", [32], F32),
        ("DMF", [32], F32), ("ONB", [128], BF), ("BA", [128], BF), ("BO", [128], BF), ("NBO", [128], BF), ("NT", [128], BF),
        ("ID", [128], BF), ("WMU", [144], BF), ("EX0", [16], F32), ("EX1", [16], F32), ("W0", [16], BF), ("W1", [16], BF),
        ("THR", [1], F32), ("CL", [264], F32), ("CI", [264], I32), ("CJ", [264], I32), ("CB", [264], F32),
        ("LB", [2, 256], BF), ("HB", [2, 8], F32), ("CT0", [S + 64], BF), ("CT1", [S + 64], BF),
        ("F2V", [416], F32), ("L128", [128], F32), ("BLF", [16], F32), ("BL", [16], U16), ("ON32", [32], F32),
):
    _sb(_n, _s, _d)
for _t in range(3):
    for _n, _s, _d in (("LI", [2, L], U16), ("KA", [L], F32), ("ZL", [L], BF), ("Z16", [13, 256], BF),
                       ("DU", [16], F32), ("DS", [16], F32), ("DT", [16], U16), ("LW", [80 + 1024], F32),
                       ("PL", [32], U16), ("LU", [16], U16)):
        if not (_t == 0 and _n in ("ZL", "LW", "PL", "LU")):
            _sb("%s%d" % (_n, _t), _s, _d)
for _d, _w in _fill.items():
    SCRATCH["S" + _d] = ("sbuf", [128, _w], _d)
for _n in ["PH", "PF"] + ["T%d" % i for i in range(6)]:
    SCRATCH[_n] = ("psum", [128, 512], F32)
    PLACE[_n] = (_n, 0, 512)


def plan(T, topo):
    n = len(T.cores)
    out = {}
    for r in range(n):
        src = T.cores[r]
        for m in MSGS:
            dst = T.cores[(r + TO[m]) % n]
            relay = None
            if not topo.may_write(src, dst):
                c = [x for x in topo.cores_of(src) if x != src and topo.may_write(x, dst) and topo.die(x) == topo.die(src)]
                relay = c[0] if m == "F3" else c[-1]
            out[(r, m)] = (src, relay, dst)
    return out


def engines(topo, a, b, m):
    e = topo.engines(a, b)
    if m in TABLES:
        return e[:4] if len(e) == 8 else e[8:12]
    return e[4:8]


def bits(e):
    return sum(1 << x for x in e)


def land(T, m):
    return T[m][:, 0:S] if m in TABLES else T[m][:, :]


def relay_program(g, core, T, topo, pl):
    todo = sorted((ORDER.index(m), m, r) for (r, m), (s, y, d) in pl.items() if y == core)
    for _, m, r in todo:
        s, y, d = pl[(r, m)]
        g.wait_ge(T.sem["a_" + m], len(engines(topo, s, y, m)))
        rid, pid = topo.addr(d, y)
        g.remote_dma(land(T, m), land(T, m), T.sem["a_" + m], T.sem["l_" + m], pid, rid, bits(engines(topo, y, d, m)))
    for _, m, r in todo:
        s, y, d = pl[(r, m)]
        g.wait_ge(T.sem["l_" + m], len(engines(topo, y, d, m)))


def rank_program(g, core, T, topo):
    pl = plan(T, topo)
    rank = T.rank_of(core)
    if rank is None:
        return relay_program(g, core, T, topo, pl)
    Q = {"V": g.vector, "A": g.scalar, "P": g.tensor, "G": g, "S": g.sync}
    cnt = {}
    know = {e: {} for e in Q}
    know["net"] = {}
    hist = {}

    def b(name, lo=0, hi=None, step=1, p=(0, 128)):
        name, first, width = PLACE[name]
        hi = first + (width if hi is None else hi)
        lo += first
        ap = T[name][p[0]:p[1], lo:hi] if step == 1 else T[name][p[0]:p[1], lo:hi:step]
        return (ap, name, (0, 1, lo, hi), None, -(-(hi - lo) // step))

    def b3(name, c0, c1, lo, hi, p=(0, 128)):
        return (T[name][p[0]:p[1], c0:c1, lo:hi], name, (c0, c1, lo, hi), None, (c1 - c0) * (hi - lo))

    def b2(name, c, lo, hi, p=(0, 128)):
        return (T[name][p[0]:p[1], c, lo:hi], name, (c, c + 1, lo, hi), None, hi - lo)

    def ind(win, off):
        return (win[0].indirect(off[0]), win[1], win[2], off, 16 * off[4])

    def hits(x, y):
        return x[0] < y[1] and y[0] < x[1] and x[2] < y[3] and y[2] < x[3]

    def inside(x, y):
        return x[0] >= y[0] and x[1] <= y[1] and x[2] >= y[2] and x[3] <= y[3]

    def regions(ops):
        return [(o[1], o[2], SCRATCH[o[1]][0] == "psum") for o in ops if isinstance(o, tuple)]

    def offsets(ops):
        return [o[3] for o in ops if isinstance(o, tuple) and o[3]]

    def sync(e, reads, writes):
        deps = {}
        for w, lst in ((False, reads), (True, writes)):
            for name, reg, psum in lst:
                for (r2, w2, e2, sem, count, snap) in hist.get(name, []):
                    if not (psum and e2 != e):
                        if not (w or w2) or not hits(reg, r2):
                            continue
                        if e2 == e and (e == "P" or not w2) and e in ENG:
                            continue
                    if deps.get(sem, (0, None))[0] < count:
                        deps[sem] = (count, snap)
        k = know[e]
        for sem in sorted(deps, key=lambda x: -len(deps[x][1])):
            count, snap = deps[sem]
            if k.get(sem, 0) < count:
                Q[e].wait_ge(T.sem[sem], count)
                k[sem] = count
                for s2, v in snap.items():
                    if k.get(s2, 0) < v:
                        k[s2] = v

    def note(e, reads, writes, sem, n):
        cnt[sem] = cnt.get(sem, 0) + n
        snap = dict(know[e])
        for w, lst in ((False, reads), (True, writes)):
            for name, reg, psum in lst:
                keep = [x for x in hist.get(name, [])
                        if not (inside(x[0], reg) and (w or (not x[1] and x[2] == e and x[3] == sem)))]
                hist[name] = keep + [(reg, w, e, sem, cnt[sem], snap)]

    def emit(e, f, out, ins):
        reads, writes = regions(ins + offsets(ins + [out])), regions([out])
        sync(e, reads, writes)
        f(Q[e]).then_inc(T.sem["q" + e], 1)
        note(e, reads, writes, "q" + e, 1)

    nodes, seen, group = [], {}, []

    def node(e, run, reads, writes, dur, lat=0.0, after=None):
        k, before = len(nodes), {}
        if after is not None:
            before[after] = 1
        for w, lst in ((False, reads), (True, writes)):
            for name, reg, psum in lst:
                for (r2, w2, j) in seen.get(name, []):
                    if nodes[j][0] == e == "P" and psum:
                        if hits(reg, r2):
                            before.setdefault(j, 0)
                    elif (psum and nodes[j][0] != e) or ((w or w2) and hits(reg, r2)):
                        before[j] = max(before.get(j, 0), 1 if w2 or nodes[j][0] != e else 0)
        for w, lst in ((False, reads), (True, writes)):
            for name, reg, psum in lst:
                keep = [x for x in seen.get(name, []) if not (w and inside(x[0], reg) and not psum)]
                seen[name] = keep + [(reg, w, k)]
        nodes.append((e, run, dur, lat, sorted(before.items())))
        return k

    def op(e, f, out, ins, after=None):
        win = [x for x in ins if isinstance(x, tuple) and x[3]]
        c = 0.00083 * max(x[4] for x in ins + [out] if isinstance(x, tuple))
        if e == "G":
            dur = 0.15 + 2 * c
        elif out[3]:
            dur = 0.05 + 3.5 * c
        elif win:
            dur = 0.06 + 1.56 * 0.00083 * out[4]
        else:
            two = all(SCRATCH[x[1]][2] in (BF, U16) for x in ins + [out] if isinstance(x, tuple))
            both = len(ins) == 2 and all(isinstance(x, tuple) and x[4] == out[4] and SCRATCH[x[1]][0] == "sbuf" for x in ins)
            dur = max(0.06, 0.05 + c * (0.5 if two else 2 if both else 1)) + (0.14 if e == "A" else 0)
        node(e, lambda: emit(e, f, out, ins), regions(ins + offsets(ins + [out])), regions([out]), dur, 0.0, after)

    def issue():
        tail, left, free, end, succ = [0.0] * len(nodes), [len(x[4]) for x in nodes], {}, {}, [[] for _ in nodes]
        for k, x in enumerate(nodes):
            for j, full in x[4]:
                succ[j].append((k, full))
        for k in reversed(range(len(nodes))):
            tail[k] = nodes[k][2] + max([0.0] + [tail[s] + (nodes[k][3] + LAG) * full for s, full in succ[k]])
        ready, order = [k for k in range(len(nodes)) if not left[k]], []
        while ready:
            start, first = {}, {}
            for k in ready:
                e, run, dur, lat, before = nodes[k]
                start[k] = max([free.get(e, 0.0)] + [end[j] - (0 if full else nodes[j][3]) + LAG * full for j, full in before])
                first[e] = min(first.get(e, 1e9), start[k])
            e = min(first, key=lambda x: first[x])
            k = max((k for k in ready if nodes[k][0] == e and start[k] <= first[e] + SLACK), key=lambda k: (tail[k], -k))
            ready.remove(k)
            order.append(k)
            free[e] = start[k] + nodes[k][2]
            end[k] = free[e] + nodes[k][3]
            for s, full in succ[k]:
                left[s] -= 1
                if not left[s]:
                    ready.append(s)
        for k in order:
            nodes[k][1]()

    def A_(o):
        return o[0] if isinstance(o, tuple) else o

    def tt(out, a, c, o):
        op("V", lambda q: q.tensor_tensor(A_(out), A_(a), A_(c), o), out, [a, c])

    def ts(out, a, s1, o1, s2=None, o2=None):
        if o2 is None:
            op("V", lambda q: q.tensor_scalar(A_(out), A_(a), A_(s1), None, o1), out, [a, s1])
        else:
            op("V", lambda q: q.tensor_scalar(A_(out), A_(a), A_(s1), A_(s2), o1, o2), out, [a, s1, s2])

    def cp(out, a):
        op("V", lambda q: q.tensor_copy(A_(out), A_(a)), out, [a])

    def scan(out, d0, d1, o0, o1):
        op("V", lambda q: q.tensor_tensor_scan(A_(out), A_(d0), A_(d1), 0.0, o0, o1), out, [d0, d1])

    def ms(out, v):
        op("V", lambda q: q.memset(A_(out), v), out, [])

    def act(out, a, fn=AF.Copy, scale=1.0, bias=0.0):
        op("A", lambda q: q.activation(A_(out), A_(a), fn, bias=A_(bias), scale=A_(scale)), out, [a, scale, bias])

    tiles = {}

    def mm_now(out, l, r, st, sp, tile):
        was = tiles.get(out[1], (tile, 0))
        if tile is not None and was[0] != tile and know["P"].get("qP", 0) < was[1]:
            g.tensor.wait_ge(T.sem.qP, was[1])
            know["P"]["qP"] = was[1]
        emit("P", lambda q: q.matmul(A_(out), A_(l), A_(r), st, sp), out, [l, r])
        tiles[out[1]] = (tile, cnt["qP"])

    def mm(out, l, r, st, sp, tile=None):
        group.append((out, l, r, st, sp, tile))
        if sp and not group[0][0] == "open":
            close()

    def close():
        m = [x for x in group if x[0] != "open"]
        group.clear()
        node("P", lambda: [mm_now(*x) for x in m], regions([x[1] for x in m] + [x[2] for x in m]), regions([x[0] for x in m]),
             sum(0.02 + 0.00042 * max(64, x[0][4]) for x in m))

    def iota(out, pat, base, cm, after=None):
        if SCRATCH[out[1]][2] == I32:
            op("G", lambda q: q.iota(A_(out), pat, base, cm), out, [], after)
        else:
            op("G", lambda q: q.iota(A_(out), pat, base, cm, allow_small_or_imprecise_dtypes=True), out, [], after)

    def asel(out, a, pat, o, base, cm):
        op("G", lambda q: q.affine_select(A_(out), A_(a), pat, o, 0.0, base, cm), out, [a])

    def scat(win, width, off, n, val):
        cp(ind(b(win, 0, width), b(off, 0, n)), val)

    def load(e, out, src, name):
        w = regions([out])

        def run():
            sync(e, [], w)
            Q[e].dma_start(out[0], src).then_inc(T.sem["d_" + name], 16)
            note(e, [], w, "d_" + name, 16)
        node(e, run, [], w, 0.1, 3.4 if out[4] > 700 else 2.4)

    def store(e, dst, a, name):
        r = regions([a])

        def run():
            sync(e, r, [])
            Q[e].dma_start(dst, a[0]).then_inc(T.sem["o_" + name], 16)
            note(e, r, [], "o_" + name, 16)
        node(e, run, r, [], 0.1, 5.0 if name == "yt" else 2.0)

    def send(m, src):
        s, y, d = pl[(rank, m)]
        to = d if y is None else y
        r = regions([src])
        es = engines(topo, core, to, m)
        rid, pid = topo.addr(to, core)

        def run():
            sync("G", r, [])
            g.remote_dma(land(T, m), src[0], T.sem["a_" + m], T.sem["l_" + m], pid, rid, bits(es))
            note("G", r, [], "l_" + m, len(es))
        k = node("G", run, r, [], 0.1)
        for (r_, m_), (s_, y_, d_) in pl.items():
            if d_ == core and m_ == m:
                w = regions([b(m, 0, S) if m in TABLES else b(m)])
                n = len(engines(topo, s_ if y_ is None else y_, d_, m))
                lat = (1.7 + (9.0 if m in TABLES else 0.8 if src[4] > 100 else 0.0)) * (1 if y_ is None else 2)
                node("n" + m, lambda: note("net", [], w, "a_" + m, n), [], w, 0.0, lat, k)
        return k

    load("S", b("EFI", 0, L), T.ef[:, 0:L], "ef0")
    load("A", b("HT", 0, S), T.tab[:, :], "tab")
    load("S", b("EHI", 0, L), T.eh[:, 0:L], "eh0")
    load("S", b("ZF", 0, L), T.zf[:, 0:L], "zf0")
    load("S", b("TC"), T.tab[:, :], "tc")
    load("S", b("EFI", L, F), T.ef[:, L:F], "ef1")
    load("S", b("EHI", L, F), T.eh[:, L:F], "eh1")
    load("S", b("ZF", L, F), T.zf[:, L:F], "zf1")

    ms(b("ONB"), 1.0)
    iota(b("PI"), [[0, 1]], 0, 1)
    iota(b("KIO"), [[0, 13], [1, 16]], 0, 0)
    asel(b("BA"), b("ONB"), [[-16, 8], [0, 16]], OP.is_ge, 0, 1)
    asel(b("BO"), b("BA"), [[16, 8], [0, 16]], OP.is_ge, 15, -1)
    asel(b("ID"), b("ONB"), [[-1, 128]], OP.is_equal, 0, 1)
    iota(b("EX0", 0, 13), [[16, 13]], 0, -1)
    iota(b("EX1", 0, 13), [[16, 13]], -NB, -1)
    ts(b("PJ"), b("PI"), 15, OP.bitwise_and)
    ts(b("PK"), b("PI"), 4, OP.arith_shift_right, 1, OP.bitwise_and)
    cp(b("PM"), b("PJ"))
    cp(b("MH1"), b("PK"))
    ts(b("MH0"), b("MH1"), -1.0, OP.mult, 1.0, OP.add)
    ts(b("PW"), b("PM"), -1.0, OP.mult, 11.0, OP.add)
    act(b("PW"), b("PW"), AF.Exp, LN2)
    for x in (0, 1):
        ex = "EX%d" % x
        ts(b(ex, 0, 13), b(ex, 0, 13), 60.0, OP.min, -60.0, OP.max)
        act(b("W%d" % x, 0, 13), b(ex, 0, 13), AF.Exp, LN2)
    ts(b("THR"), b("PW"), 2.5 / 2048.0, OP.mult)
    ms(b("MB", 0, 1), 200.0)
    ms(b("MB", 1, 2), -10.0)
    ms(b("WMU"), 0.0)
    ts(b("WMU", 15, 143, 16), b("BO", 0, 128, 16), float(PEN), OP.mult)
    ts(b("NBO"), b("BO"), -1.0, OP.mult)
    ts(b("KAD"), b("KIO"), -2048.0, OP.mult, 30720.0, OP.add)
    ts(b("RKM"), b("KIO"), 0.0, OP.is_gt)
    ts(b("M16"), b("KIO"), b("PM"), OP.is_equal)

    def pack(lo, hi):
        ts(b("EE", lo, hi), b("EFI", lo, hi), 4096.0, OP.mult)
        tt(b("EE", lo, hi), b("EE", lo, hi), b("EHI", lo, hi), OP.add)

    def lists(x, c0, c1, t):
        n0, n1 = 16 * c0, 16 * c1
        ts(b3("I3", c0, c1, 0, 16), x, b("MH0"), OP.mult)
        act(b3("I3", c0, c1, 16, 32), x, scale=b("MH1"))
        y, i3 = b3("Y3", c0, c1, 0, 32), b3("I3", c0, c1, 0, 32)
        op("V", lambda q: q.transpose(T.Y3[:, c0:c1, :], T.I3[:, c0:c1, :]), y, [i3])
        tt(b3("XI", c0, c1, 0, 16), b3("Y3", c0, c1, 0, 16), b3("Y3", c0, c1, 16, 32), OP.add)
        ts(b2("HF", 0, n0, n1), b3("XI", c0, c1, 0, 16), 2047, OP.bitwise_and)
        ts(b2("HF", 1, n0, n1), b3("XI", c0, c1, 0, 16), 12, OP.arith_shift_right, 2047, OP.bitwise_and)
        cp(b3("LI%d" % t, 0, 2, n0, n1), b3("HF", 0, 2, n0, n1))

    def half(t, x):
        return lambda lo, hi: b2("LI%d" % t, x, lo, hi)

    def keyadd(c0, c1, t):
        n0, n1 = 16 * c0, 16 * c1
        tt(b("KA%d" % t, n0, n1), b("KAD", n0, n1), b2("HF", 0, n0, n1), OP.add)

    def expand(z, src, c0, c1, cp=cp):
        cp(b3(z, c0, c1, 0, 16), src)
        for w in (16, 32, 64, 128):
            cp(b3(z, c0, c1, w, 2 * w), b3(z, c0, c1, 0, w))

    bank = [0]

    def bulk(win, lst, z, cm, vch, ach):
        for c0, c1 in ach:
            w = 256 * (c1 - c0)
            ga, t = "GA%d" % (bank[0] % 3), "T%d" % (bank[0] % 6)
            bank[0] += 1
            act(b(ga, 0, w), ind(b(win, 0, S), lst(16 * c0, 16 * c1)), scale=-1.0)
            mm(b(t, 0, w), b("ID"), b3(z, c0, c1, 0, 256), True, False)
            mm(b(t, 0, w), b("ID"), b(ga, 0, w), False, True)
            act(b(cm, 256 * c0, 256 * c1), b(t, 0, w), AF.Sigmoid, 400.0, b("MB", 0, 1))
        for c0, c1 in vch:
            for c in range(c0, c1):
                tt(b(cm, 256 * c, 256 * c + 256), ind(b(win, 0, S), lst(16 * c, 16 * c + 16)), b2(z, c, 0, 256), OP.is_le)

    def psum(cm, dst, *cuts):
        for c0, c1 in zip(cuts, cuts[1:]):
            for m in range(16):
                mm(b(dst, 16 * c0, 16 * c1), b("WMU", 15 - m, 143 - m), b(cm, 256 * c0 + m, 256 * c1, 16), m == 0, m == 15)

    def home_max(t):
        tt(b("HK"), b("PH", 0, L), b("KA%d" % t), OP.add)
        scan(b("HS"), b("RKM"), b("HK"), OP.mult, OP.max)
        cp(b("HKI", 0, 13), b("HS", 15, L, 16))
        ts(b("HSL", 0, 13), b("HKI", 0, 13), 2047, OP.bitwise_and)
        ts(b("A1", 0, 13), b("HKI", 0, 13), float(9 * PEN), OP.is_ge, float(9 * PEN), OP.mult)
        ts(b("AP", 0, 13), b("HSL", 0, 13), float(OKB), OP.add)
        tt(b("AP", 0, 13), b("AP", 0, 13), b("A1", 0, 13), OP.max)

    JOBS = []
    for h in (0, 1):
        for a in (h, 2 + h):
            JOBS += [(2 * a, "T%d" % a, 0, 0), (2 * a + 1, "T%d" % a, L, 0)]
        JOBS += [(2 * h + x, "T4", 192 * h + 96 * x, 1) for x in (0, 1)]
        JOBS += [(4 + 2 * h + x, ("T5", "PF")[h], L * h + 96 * x, 1) for x in (0, 1)]

    def decide(t, kf):
        tt(b("YY", 0, 13), b("AP", 0, 13), kf, OP.max)
        ts(b("IX", 0, 13), b("YY", 0, 13), float(OKB + S), OP.min, float(OKB), OP.subtract)
        act(b("B1"), ind(b("CT1", 0, S + 16), b("IX", 0, 13)))
        cp(b("B0"), ind(b("CT0", 0, S + 16), b("IX", 0, 13)))
        for gg, t_, o, blk in JOBS:
            pp, lo, n = (32 * (gg // 2), 32 * (gg // 2) + 32), (0, NB)[blk], (NB, 96)[blk]
            bb = "B%d" % (gg % 2)
            mm(b(t_, o, o + L - lo, p=(0, n)), b(bb, lo, lo + n, p=pp), b(bb, lo, L, p=pp), True, True, gg // 2)
        for gg, t_, o, blk in JOBS:
            w, pp = (L, 96)[blk], (0, (NB, 96)[blk])
            out = b3("E%d" % blk, 0, (13, 6)[blk], 16 * gg, 16 * gg + 16, p=pp)
            if t_ in ("T2", "T3", "PF"):
                act(out, b(t_, o, o + w, p=pp), AF.Relu, 1.0, b("MB", 1, 2, p=pp))
            else:
                ts(out, b(t_, o, o + w, p=pp), 10.5, OP.is_ge)
        ts(b("D0", 0, 13), b("YY", 0, 13), float(-OKB), OP.add)
        group.append(("open",))
        for c in range(13):
            mm(b("PH", 416 + c, 417 + c), b2("E0", c, 0, 128, p=(0, NB)), b("W0", c, c + 1, p=(0, NB)), True, c < 7)
            if c >= 7:
                mm(b("PH", 416 + c, 417 + c), b2("E1", c - 7, 0, 128, p=(0, 96)), b("W1", c, c + 1, p=(0, 96)), False, True)
        close()
        tt(b("WM", 0, 13), b("HS", 15, L, 16), kf, OP.max)
        cp(b("WI", 0, 13), b("WM", 0, 13))
        ts(b("WS", 0, 13), b("WI", 0, 13), 15, OP.arith_shift_right)
        ts(b("WR", 0, 13), b("WS", 0, 13), 9.0, OP.is_ge)
        tt(b("WV", 0, 13), b("WR", 0, 13), b("WS", 0, 13), OP.mult)
        tt(b("XB"), ind(b("WV", 0, 16), b("BL", 0, 13)), b("M16"), OP.mult)
        mm(b("PF", L, 2 * L), b("BO"), b("XB"), True, True)
        ts(b("L1", 0, 13), b("PH", 416, 429), b("THR"), OP.is_gt, 4096.0, OP.mult)
        tt(b("D2", 0, 13), b("L1", 0, 13), b("D0", 0, 13), OP.max)
        tt(b("DS%d" % t, 0, 13), b("D2", 0, 13), b("DU%d" % t, 0, 13), OP.min)
        cp(b("DT%d" % t, 0, 13), b("DS%d" % t, 0, 13))

    def ranks(n):
        scan(b("UC", 0, n), b("ON32", 0, n), b("UU", 0, n), OP.mult, OP.add)
        group.append(("open",))
        mm(b("PF", 416, 416 + n), b("BO"), b("UC", 0, n), True, False)
        mm(b("PF", 416, 416 + n), b("NT"), b("UU", 0, n), False, True)
        mm(b("PF", 448, 449), b("BO"), b("UC", n - 1, n), True, True)
        close()

    def lanes(t, n, fill, val):
        pls, lw, lu = "PL%d" % t, "LW%d" % t, "LU%d" % t
        ts(b("TB"), b("PF", 448, 449), -1.0, OP.mult, float(fill), OP.add)
        tt(b("QQ", 0, n), b("PF", 416, 416 + n), b("NU", 0, n), OP.max)
        cp(b(pls, 0, n), b("QQ", 0, n))
        act(b(lw, 80, 208), b("L128"), AF.Identity, 1.0, b("TB"))
        cp(ind(b(lw, 80, 80 + 1024), b(pls, 0, n)), val)
        tt(b("XM"), b(lw, 80, 208), b("M16", 0, 128), OP.mult)
        scan(b("XS"), b("RKM", 0, 128), b("XM"), OP.mult, OP.add)
        cp(b(lu, 0, 8), b("XS", 15, 128, 16))

    AS, VS = [(0, 2), (2, 3)], [(3, 5)]
    AD, VD = [(9, 11), (5, 6)], [(6, 9), (11, 13)]
    A0, V0 = [(0, 2), (2, 3), (9, 11)], [(3, 9), (11, 13)]

    def step(t, ftab, update, later):
        lu, hl, fl, z = "LU%d" % t, half(t, 0), half(t, 1), "Z16%d" % t
        bulk("HT", hl, z, "CMH", VS, AS)
        act(b("DQ"), ind(b("D"), b(lu, 0, 8)), scale=4097.0)
        act(b("ZL%d" % t, 80, L), ind(b("ZF"), b(lu, 0, 8)))
        tt(b("XE"), ind(b("EE"), b(lu, 0, 8)), b("DQ"), OP.add)
        lists(b("XE"), 5, 13, t)
        update()
        bulk(ftab, fl, z, "CMF", VS, AS)
        psum("CMH", "PH", 0, 5)
        expand(z, b("ZL%d" % t, 80, L), 5, 13)
        keyadd(5, 13, t)
        bulk("HT", hl, z, "CMH", VD, AD)
        psum("CMF", "PF", 0, 5)
        bulk(ftab, fl, z, "CMF", VD, AD)
        psum("CMH", "PH", 5, 9, 13)
        psum("CMF", "PF", 5, 9)
        home_max(t)
        psum("CMF", "PF", 9, 13)
        later()
        scan(b("FS"), b("RKM"), b("PF", 0, L), OP.mult, OP.max)
        decide(t, b("FS", 15, L, 16))

    send("RQZ", b("ZF", 0, L))
    send("U3Z", b("ZF", 0, L))
    send("U2Z", b("ZF", 0, L))
    pack(0, L)
    lists(b("EE", 0, L), 0, 13, 0)
    asked = send("RQL", b2("LI0", 1, 0, L))
    expand("Z160", b("ZF", 0, L), 0, 13)
    keyadd(0, 13, 0)
    send("F2", b("TC"))
    send("F3", b("TC"))
    asel(b("NT"), b("NBO"), [[-1, 128]], OP.is_ge, 0, 1)
    iota(b("CL", 0, 256), [[1, 256]], 0, 0)
    iota(b("CL", 256, 264), [[256, 8]], 0, 0)
    iota(b("C16", 0, 26), [[16, 26]], 0, 0)
    iota(b("BLF", 0, 13), [[1, 13]], 0, 0)
    iota(b("F2V", 0, 80), [[1, 80]], 544, 0)
    iota(b("F2V", 80, 416), [[1, 336]], 0, 0, asked)
    bulk("HT", half(0, 0), "Z160", "CMH", V0, A0)
    expand("ZR", b("RQZ"), 0, 13)
    bulk("HT", lambda lo, hi: b("RQL", lo, hi), "ZR", "CMF", V0, A0)
    psum("CMH", "PH", 0, 5, 9, 13)
    psum("CMF", "PF", 0, 5, 9, 13)
    cp(b("PX"), b("PW"))
    cp(b("PY"), b("PX"))
    ts(b("CI"), b("CL"), b("PY"), OP.mult)
    ts(b("CJ"), b("CI"), 2048, OP.bitwise_and)
    ts(b("CB"), b("CJ"), 1.0 / 1024.0, OP.mult, -1.0, OP.add)
    ts(b("ML", 2, 3), b("PM"), 8.0, OP.is_lt)
    ts(b("MH", 2, 3), b("PM"), 11.0, OP.is_lt)
    tt(b("MH", 2, 3), b("MH", 2, 3), b("ML", 2, 3), OP.subtract)
    for x in (0, 1):
        tt(b("ML", x, x + 1), b("ML", 2, 3), b("MH%d" % x), OP.mult)
        tt(b("MH", x, x + 1), b("MH", 2, 3), b("MH%d" % x), OP.mult)
        ts(b2("LB", x, 0, 256), b("CB", 0, 256), b("ML", x, x + 1), OP.mult)
        ts(b2("HB", x, 0, 8), b("CB", 256, 264), b("MH", x, x + 1), OP.mult)
        ms(b("CT%d" % x, S, S + 16), 0.0)
    ms(b("KFO"), 0.0)
    scan(b("FS"), b("RKM"), b("PF", 0, L), OP.mult, OP.max)
    cp(b("KFO", 0, 13), b("FS", 15, L, 16))
    told = send("KFR", b("KFO"))
    home_max(0)
    iota(b("LW1", 0, 80), [[1, 80]], 544, 0, told)
    iota(b("LW2", 0, 80), [[1, 80]], 464, 0, told)
    iota(b("L128"), [[1, 128]], 0, 0)
    for x in range(0, WT, 704):
        iota(b("OC", x, x + 704), [[0, 704]], -1, 0, told)
    for x in (0, 512):
        iota(b("LVF", x, x + 512), [[0, 512]], x // 8, 0, told)
        iota(b("LVW", x, x + 512), [[0, 512]], 0, 0, told)
    for h in range(8):
        act(b("CT1", 256 * h, 256 * h + 256), b2("LB", 1, 0, 256), AF.Identity, 1.0, b2("HB", 1, h, h + 1))
        ts(b("CT0", 256 * h, 256 * h + 256), b2("LB", 0, 0, 256), b2("HB", 0, h, h + 1), OP.add)
    ts(b("FW", 0, 26), b("C16", 0, 26), b("PM"), OP.add)
    for t in range(3):
        ts(b("DU%d" % t, 0, 13), b("FW", 0, 13), float(S + 256 * t), OP.add)
    ts(b("DMF", 0, 26), b("FW", 0, 26), 512.0, OP.add)
    cp(b("BL", 0, 13), b("BLF", 0, 13))
    for n_, v_ in (("WV", 0.0), ("WN", 0.0), ("DT0", 0), ("DT1", 0), ("ON32", 1.0), ("D", 0.0), ("BP", 0.0)):
        ms(b(n_), v_)
    pack(L, F)
    for t, f0 in ((1, 544), (2, 464)):
        lists(b("EE", f0, f0 + 80), 0, 5, t)
        keyadd(0, 5, t)
        act(b("ZL%d" % t, 0, 80), b("ZF", f0, f0 + 80))
        expand("Z16%d" % t, b("ZF", f0, f0 + 80), 0, 5, act)
    decide(0, b("KFR", 0, 13))
    send("U2D", b("DT0"))
    send("U3D", b("DT0"))

    ts(b("UU", 0, 13), b("DS0", 0, 13), float(S), OP.is_ge)
    ranks(13)
    ts(b("NU", 0, 13), b("DS0", 0, 13), float(S), OP.is_lt)
    tt(b("NU", 0, 13), b("NU", 0, 13), b("DMF", 0, 13), OP.mult)
    scat("HT", WT, "DT0", 13, b("ZF", 0, L))
    lanes(1, 13, 208, b("F2V", 80, 288))
    act(b("D", 0, L), b("PF", L, 2 * L))

    def update1():
        send("V3Z", b("ZL1"))
        scat("F2", WT, "U2D", 13, b("U2Z"))

    def later1():
        scat("OC", WT, "DT0", 13, b("F2V", 80, 288))
        scat("F3", WT, "U3D", 13, b("U3Z"))
    step(1, "F2", update1, later1)
    send("V3D", b("DT1"))

    ts(b("WN", 0, 13), b("DS1", 0, 13), float(S), OP.is_lt, 64.0, OP.mult)
    tt(b("XB"), ind(b("WN", 0, 16), b("BL", 0, 13)), b("M16"), OP.mult)
    mm(b("PH", L, 2 * L), b("BO"), b("XB"), True, True)
    act(b("LVF", 0, 128), b("PH", L + 80, 2 * L))
    act(b("LVW", 0, 128), b("PF", L + 80, 2 * L))
    act(b("D", 544, F), b("PF", L, L + 80))
    ts(b("TU"), b("TB"), -1.0, OP.mult)
    ts(b("PL1", 13, 21), b("FW", 13, 21), b("TU"), OP.add)
    scat("OC", WT, "DT1", 13, b("LW1", 0, L))
    tt(b("BP", 0, L), ind(b("OC"), b("DT0", 0, 13)), b("F2V", 80, 288), OP.not_equal)
    ts(b("UF"), ind(b("LVF"), b("PL1", 0, 21)), 64.0, OP.is_lt)
    for x in ("BP", "UF"):
        for m in range(16):
            mm(b("PH", 450, 471), b("WMU", 15 - m, 143 - m), b(x, m, 336, 16), x == "BP" and m == 0, x == "UF" and m == 15)
    ts(b("UU", 0, 5), b("DS1", 0, 5), float(S), OP.is_ge)
    scat("HT", WT, "DT1", 13, b("ZL1"))
    act(b("GW"), ind(b("LVW"), b("PL1", 0, 21)))
    ts(b("UU", 5, 26), b("PH", 450, 471), 1.0, OP.is_ge)
    ranks(26)
    ts(b("NU", 0, 26), b("UU", 0, 26), -1.0, OP.mult, 1.0, OP.add)
    tt(b("NU", 0, 26), b("NU", 0, 26), b("DMF", 0, 26), OP.mult)
    lanes(2, 26, 336, b("F2V"))
    for i, x in enumerate(("D", "GW", "BP")):
        mm(b("T5", 0, 336), b("ID"), b(x, 0, 336), i == 0, i == 2)
    act(b("D", 0, 336), b("T5", 0, 336))

    def later2():
        ts(b("NB1"), b("BP", 0, L), -1.0, OP.mult, 1.0, OP.add)
        act(b("DL"), ind(b("D"), b("LU2", 0, 8)))
        ms(b("DF", 336, 464), 0.0)
    step(2, "F3", lambda: scat("F3", WT, "V3D", 13, b("V3Z")), later2)

    scat("HT", WT, "DT2", 13, b("ZL2"))
    store("S", T.yt[:, :], b("HT", 0, S), "yt")
    scat("OC", WT, "DT2", 13, b("LW2", 0, L))
    store("A", T.yo[:, :], (T.OC[0:128:16, 0:S], "OC", (0, 1, 0, S), None, S), "yo")
    tt(b("B3"), ind(b("OC"), b("DT0", 0, 13)), b("F2V", 80, 288), OP.not_equal)
    tt(b("HK"), ind(b("OC"), b("DT1", 0, 13)), b("LW1", 0, L), OP.not_equal)
    tt(b("BP", 0, L), b("B3"), b("NB1"), OP.mult)
    cp(b("LVW", 0, 128), b("HK", 80, L))
    cp(b("B2"), ind(b("LVW"), b("PL1", 0, 21)))
    for i, x in enumerate(("D", "BP", "B2")):
        mm(b("T4", 0, 336), b("ID"), b(x, 0, 336), i == 0, i == 2)
    tt(b("ND"), b("DL"), b("PF", L + 80, 2 * L), OP.add)
    cp(b("DF", 464, 544), b("PF", L, L + 80))
    tt(b("DF", 544, F), b("D", 544, F), b("HK", 0, 80), OP.add)
    cp(b("DF", 0, 336), b("T4", 0, 336))
    scat("DF", F, "LU2", 8, b("ND"))
    store("S", T.yd[:, :], (T.DF[0:128:16, 0:F], "DF", (0, 1, 0, F), None, F), "yd")
    issue()
    for s in SEMAPHORES:
        if s in cnt and know["G"].get(s, 0) < cnt[s]:
            g.wait_ge(T.sem[s], cnt[s])
